import numpy as np
import ml_dtypes


def mxq(x, axis, fmt="e4m3"):
    dtype, down = {"e4m3": (ml_dtypes.float8_e4m3fn, 7), "e5m2": (ml_dtypes.float8_e5m2, 14)}[fmt]
    v = np.moveaxis(np.asarray(x, np.float32).astype(ml_dtypes.bfloat16).astype(np.float64), axis, -1)
    blocks = v.reshape(v.shape[:-1] + (-1, 32))
    amax = np.abs(blocks).max(-1, keepdims=True)
    byte = np.maximum(np.where(amax > 0, np.frexp(amax)[1] - 1 + 127, 0) - down, 1)
    scale = np.exp2(byte - 127.0)
    codes = (blocks / scale).astype(np.float32).astype(dtype).astype(np.float64)
    return np.moveaxis((codes * scale).reshape(v.shape), -1, axis)


WIDE = False


def mx_kscale(k):
    if not WIDE:
        return np.ones(k)
    levels = np.array([10, -10, 5, -5, 0])
    if k % 512:
        return np.exp2(np.random.permutation(np.resize(levels, k // 32))).repeat(32)
    a = np.empty((k // 512, 16))
    for p in range(k // 512):
        a[p, :8] = np.random.permutation(np.resize(levels, 8))
        for g in range(8):
            far = levels[np.abs(levels - a[p, g]) >= 10]
            a[p, g + 8] = far[np.random.randint(len(far))]
    return np.exp2(a.ravel()).repeat(32)


def f64(x):
    return np.asarray(x).astype(np.float64)


def striped(idx):
    return np.tile(idx.reshape(-1, 16).T, (8, 1)).astype(np.uint16)


def unstriped(offs):
    return offs[:16].T.reshape(-1).astype(np.int64)


E2M1 = np.array([0.0, 0.5, 1.0, 1.5, 2.0, 3.0, 4.0, 6.0, -0.0, -0.5, -1.0, -1.5, -2.0, -3.0, -4.0, -6.0])


def pack_weight(w, fmt):
    k, n = w.shape
    w = f64(np.asarray(w, np.float32).astype(ml_dtypes.bfloat16)).reshape(k // 32, 32, n)
    amax = np.abs(w).max(1)
    if fmt == "e4m3":
        byte = np.frexp(amax)[1] - 1 + 127 - 7
    else:
        mant, ex = np.frexp(amax / 6.0)
        byte = np.where(mant > 0.5, ex, ex - 1) + 127
    byte = np.clip(np.where(amax > 0, byte, 1), 1, 254)
    scaled = (w * np.exp2(127.0 - byte)[:, None, :]).reshape(k, n).astype(np.float32)
    by_word = np.ascontiguousarray(scaled.reshape(k // 512, 128, 4, n).transpose(0, 1, 3, 2))
    if fmt == "e4m3":
        words = by_word.astype(ml_dtypes.float8_e4m3fn).view(np.uint8)
    else:
        c = by_word.astype(ml_dtypes.float4_e2m1fn).view(np.uint8) & 0xF
        words = (c[..., 0::2] | (c[..., 1::2] << 4)).reshape(k // 512, 128, 2 * n)
    return np.ascontiguousarray(words), np.ascontiguousarray(byte.astype(np.uint8).reshape(k // 512, 16, n))


def unpack_weight(words, scales, fmt):
    g, _, n = scales.shape
    words = np.ascontiguousarray(words).reshape(g, 128, n, -1)
    if fmt == "e4m3":
        vals = words.view(ml_dtypes.float8_e4m3fn).astype(np.float64)
    else:
        nib = np.empty((g, 128, n, 4), np.uint8)
        nib[..., 0::2] = words & 0xF
        nib[..., 1::2] = words >> 4
        vals = E2M1[nib]
    vals = vals * np.repeat(np.exp2(scales.astype(np.float64) - 127.0), 8, axis=1)[..., None]
    return vals.transpose(0, 1, 3, 2).reshape(g * 512, n)


def gelu(v):
    return 0.5 * v * (1.0 + np.tanh(np.sqrt(2.0 / np.pi) * (v + 0.044715 * v**3)))


K, H, N, T, S = 1536, 1024, 768, 2048, 1024

def setup_inputs():
    n = np.random.standard_normal
    s = mx_kscale(K)[:, None]
    u = mx_kscale(H)[:, None]
    tab = n((K, T)) * np.exp(0.4 * n((1, T))) * s
    tab_words, tab_scales = pack_weight(tab, "e4m3")
    w1 = n((K, H)) / np.sqrt(K) / s
    w4 = 0.4 * np.exp(1.2 * n((H, N))) / H / u
    w4_words, w4_scales = pack_weight(w4, "e2m1")
    return {
        "tab_words": tab_words,
        "tab_scales": tab_scales,
        "w1": w1.astype(np.float32),
        "w4_words": w4_words,
        "w4_scales": w4_scales,
        "gain": (np.exp(0.5 * n(H)) * u[:, 0]).astype(np.float32),
        "air": np.exp(0.3 * n(N)).astype(np.float32),
        "gT": np.exp(0.4 * n((N, T))).astype(np.float32),
        "offs": striped(np.random.permutation(T)[:S]),
    }

def reference(tab_words, tab_scales, w1, w4_words, w4_scales, gain, air, gT, offs):
    v = unpack_weight(tab_words, tab_scales, "e4m3")[:, unstriped(offs)]
    h = mxq(f64(w1), 0, "e4m3").T @ v
    z = h * h * f64(gain)[:, None]
    y = unpack_weight(w4_words, w4_scales, "e2m1").T @ mxq(z, 0, "e4m3")
    g = f64(gT)[:, unstriped(offs)]
    new = g / (f64(air)[:, None] + y)
    out = f64(gT).copy()
    out[:, unstriped(offs)] = new
    return out

@@ -1,0 +1,262 @@
+from contextlib import ExitStack
+
+import concourse.mybir as mybir
+from concourse.masks import make_identity
+
+K, H, N, T, S = 1536, 1024, 768, 2048, 1024
+FLOPS = 2 * K * H * S + 2 * H * N * S
+
+F32 = mybir.dt.float32
+BF16 = mybir.dt.bfloat16
+I32 = mybir.dt.int32
+U32 = mybir.dt.uint32
+U16 = mybir.dt.uint16
+U8 = mybir.dt.uint8
+FP8X4 = mybir.dt.float8_e4m3fn_x4
+FP4X4 = mybir.dt.float4_e2m1fn_x4
+ACT = mybir.ActivationFunctionType
+MULT = mybir.AluOpType.mult
+
+P = 128
+PACK = 4
+KP = P * PACK
+KA = K // KP
+HB = H // KP
+NC = N // P
+HALF = 512
+HALVES = S // HALF
+LIST_COLS = HALF // 16
+
+
+def tile_list_jaw_scatter_correction_kernel(
+    tc, tab_words, tab_scales, w1, w4_words, w4_scales, gain, air, gT, offs, out
+):
+    nc = tc.nc
+    with ExitStack() as ctx:
+        keep = ctx.enter_context(tc.tile_pool(name="keep", bufs=1))
+        ring = ctx.enter_context(tc.tile_pool(name="ring", bufs=2))
+        psum = ctx.enter_context(tc.psum_pool(name="psum", bufs=1))
+
+        def bank(i):
+            return psum.tile([P, HALF], F32, name="bank%d" % i)
+
+        offsets = keep.tile([P, S // 16], U16, name="offsets")
+        nc.sync.dma_start(offsets[:], offs)
+
+        tab_plane = keep.tile([P, T], U8, name="tab_plane", tag="tab_plane", align_bytes=64)
+        nc.gpsimd.memset(tab_plane[:].bitcast(I32), 0)
+        w4_plane = keep.tile([P, HB * N], U8, name="w4_plane", align_bytes=64)
+        nc.vector.memset(w4_plane[:].bitcast(I32), 0)
+        air_rows = keep.tile([P, P], F32, name="air_rows")
+        nc.gpsimd.memset(air_rows[:], 0.0)
+
+        gain_cols = keep.tile([P, HB, PACK], F32, name="gain_cols")
+        nc.gpsimd.dma_start(air_rows[0:NC, :], air.rearrange("(c p) -> c p", p=P))
+
+        w_raw, tab = {}, {}
+
+        def load_w1(a, b):
+            raw = keep.tile([P, PACK, KP], F32, name="w_raw%d%d" % (a, b))
+            rows = w1[a * KP : (a + 1) * KP, b * KP : (b + 1) * KP]
+            rows = rows.rearrange("(p j) c -> p j c", j=PACK)
+            if (a, b) == (0, 0):
+                nc.sync.dma_start(raw[:, 0:2, :], rows[:, 0:2, :])
+                nc.sync.dma_start(raw[:, 2:4, :], rows[:, 2:4, :])
+            else:
+                nc.sync.dma_start(raw[:], rows)
+            w_raw[a, b] = raw
+
+        def load_tab(a):
+            words = keep.tile([P, T], U32, name="tab%d" % a, align_bytes=64)
+            nc.sync.dma_start(
+                words[:].bitcast(I32), tab_words[a].rearrange("p n i -> p (n i)").bitcast(I32)
+            )
+            tab[a] = words
+
+        load_tab(0)
+        nc.sync.dma_start(gain_cols[:], gain.rearrange("(b p t) -> p b t", b=HB, t=PACK))
+        load_w1(0, 0)
+        for q in range(4):
+            nc.sync.dma_start(
+                tab_plane[32 * q : 32 * q + 4 * KA, :].bitcast(I32),
+                tab_scales[:, 4 * q : 4 * q + 4, :].bitcast(I32),
+            )
+        load_tab(1)
+        load_w1(1, 0)
+        load_w1(2, 0)
+        load_tab(2)
+        for a in range(KA):
+            load_w1(a, 1)
+
+        readings = []
+        w4_codes = keep.tile([P, HB * 2 * N], U8, name="w4_codes", align_bytes=64)
+        for c in range(NC):
+            rows = keep.tile([P, T], F32, name="readings%d" % c)
+            nc.sync.dma_start(rows[:], gT[c * P : (c + 1) * P, :])
+            readings.append(rows)
+            if c == NC - 1:
+                nc.sync.dma_start(
+                    w4_codes[:].bitcast(I32).rearrange("p (b w) -> p b w", b=HB),
+                    w4_words.bitcast(I32).rearrange("b p w -> p b w"),
+                )
+                for q in range(4):
+                    nc.sync.dma_start(
+                        w4_plane[32 * q : 32 * q + 4, :].bitcast(I32).rearrange("r (b w) -> r b w", b=HB),
+                        w4_scales[:, 4 * q : 4 * q + 4, :].bitcast(I32).rearrange("b r w -> r b w"),
+                    )
+
+        gain_flat = gain_cols[:].rearrange("p b t -> p (b t)")
+        gain_rsqrt = keep.tile([P, HB * PACK], F32, name="gain_rsqrt")
+        nc.scalar.activation(gain_rsqrt[:], gain_flat, ACT.Abs_reciprocal_sqrt)
+        gain_root = keep.tile([P, HB * PACK], F32, name="gain_root")
+        nc.gpsimd.tensor_tensor(gain_root[:], gain_flat, gain_rsqrt[:], MULT)
+
+        identity = keep.tile([P, P], F32, name="identity")
+        make_identity(nc, identity[:])
+        air_cols = keep.tile([P, NC], F32, name="air_cols")
+
+        v_plane = keep.tile([P, S], U8, name="v_plane", align_bytes=64)
+        nc.vector.tensor_copy(v_plane[:], tab_plane[:].indirect(offsets[:]))
+
+        w_codes, w_plane, v_words = {}, {}, {}
+
+        def round_w1(a, b, copy):
+            rounded = ring.tile([P, PACK * KP], BF16, name="w_rounded", align_bytes=64)
+            copy(
+                rounded[:].rearrange("p (t m j) -> p m j t", t=PACK, j=PACK),
+                w_raw[a, b][:].rearrange("p j (m t) -> p m j t", t=PACK),
+            )
+            return rounded
+
+        def quantise_w1(a, b, rounded):
+            codes = keep.tile([P, KP], U32, name="w_codes%d%d" % (a, b), align_bytes=64)
+            tag = "tab_plane" if (a, b) == (0, 0) else "w_plane%d%d" % (a, b)
+            plane = keep.tile([P, KP], U8, name="w_plane%d%d" % (a, b), tag=tag, align_bytes=64)
+            nc.vector.quantize_mx(out=codes[:].bitcast(FP8X4), scales=plane[:], in_=rounded[:])
+            w_codes[a, b], w_plane[a, b] = codes, plane
+
+        def gather_words(a, pieces):
+            words = keep.tile([P, S], U32, name="v_words%d" % a, align_bytes=64)
+            width = S // pieces
+            for i in range(pieces):
+                nc.vector.tensor_copy(
+                    words[:, i * width : (i + 1) * width],
+                    tab[a][:].indirect(offsets[:, i * width // 16 : (i + 1) * width // 16]),
+                )
+            v_words[a] = words
+
+        h_banks = {}
+
+        def first_product(a, b, h):
+            cols = slice(h * HALF, (h + 1) * HALF)
+            for t in range(PACK):
+                if a == 0:
+                    h_banks[b, h, t] = bank(PACK * h + t)
+                nc.tensor.matmul_mx(
+                    out=h_banks[b, h, t][:],
+                    lhsT=w_codes[a, b][:, t * P : (t + 1) * P].bitcast(FP8X4),
+                    lhsT_scale=w_plane[a, b][:, t * P : (t + 1) * P],
+                    rhs=v_words[a][:, cols].bitcast(FP8X4),
+                    rhs_scale=v_plane[4 * a : P, cols],
+                    start=(a == 0),
+                    stop=(a == KA - 1),
+                )
+
+        z_rows, z_codes, z_plane = {}, {}, {}
+
+        def energies(b, h):
+            rows = ring.tile([P, PACK, HALF], BF16, name="z_rows")
+            for t in range(PACK):
+                col = PACK * b + t
+                nc.scalar.activation(
+                    rows[:, t, :], h_banks[b, h, t][:], ACT.Square, scale=gain_root[:, col : col + 1]
+                )
+            z_rows[b, h] = rows
+
+        def quantise_z(b, h):
+            woven = ring.tile([P, PACK * HALF], BF16, name="z_woven", align_bytes=64)
+            nc.scalar.copy(
+                woven[:].rearrange("p (c i t) -> p c t i", i=4, t=PACK),
+                z_rows[b, h][:].rearrange("p t (c i) -> p c t i", i=4),
+            )
+            codes = keep.tile([P, HALF], U32, name="z_codes%d%d" % (b, h), align_bytes=64)
+            plane = keep.tile([P, HALF], U8, name="z_plane%d%d" % (b, h), align_bytes=64)
+            nc.vector.quantize_mx(out=codes[:].bitcast(FP8X4), scales=plane[:], in_=woven[:])
+            z_codes[b, h], z_plane[b, h] = codes, plane
+
+        picked = {}
+
+        def gather_readings(c):
+            values = keep.tile([P, S], F32, name="picked%d" % c)
+            nc.vector.tensor_copy(values[:], readings[c][:].indirect(offsets[:]))
+            picked[c] = values
+
+        inverse = {}
+
+        def second_product(c, h, i):
+            y_bank = bank(i)
+            for b in range(HB):
+                nc.tensor.matmul_mx(
+                    out=y_bank[:],
+                    lhsT=w4_codes[:, 2 * (b * N + c * P) : 2 * (b * N + (c + 1) * P)].bitcast(FP4X4),
+                    lhsT_scale=w4_plane[:, b * N + c * P : b * N + (c + 1) * P],
+                    rhs=z_codes[b, h][:].bitcast(FP8X4),
+                    rhs_scale=z_plane[b, h][:],
+                    start=(b == 0),
+                    stop=(b == HB - 1),
+                )
+            root = ring.tile([P, HALF], F32, name="root")
+            nc.scalar.activation(root[:], y_bank[:], ACT.Abs_reciprocal_sqrt, bias=air_cols[:, c : c + 1])
+            if h == 0:
+                inverse[c] = ring.tile([P, S], F32, name="inverse", bufs=4)
+            nc.scalar.activation(inverse[c][:, h * HALF : (h + 1) * HALF], root[:], ACT.Square)
+
+        def scatter(c, first, count):
+            cols = slice(first * HALF, (first + count) * HALF)
+            nc.vector.tensor_tensor(
+                readings[c][:].indirect(offsets[:, first * LIST_COLS : (first + count) * LIST_COLS]),
+                picked[c][:, cols],
+                inverse[c][:, cols],
+                MULT,
+            )
+
+        def store(c):
+            nc.sync.dma_start(out[c * P : (c + 1) * P, :], readings[c][:])
+
+        for a in range(KA):
+            quantise_w1(a, 0, round_w1(a, 0, nc.vector.tensor_copy if a == 1 else nc.scalar.copy))
+            gather_words(a, 2 if a == KA - 1 else 1)
+            for h in range(HALVES):
+                first_product(a, 0, h)
+        energies(0, 0)
+        quantise_z(0, 0)
+        energies(0, 1)
+        air_bank = bank(PACK)
+        nc.tensor.transpose(air_bank[:, 0:P], air_rows[:], identity[:])
+        nc.scalar.copy(air_cols[:], air_bank[:, 0:NC])
+        for a in range(KA):
+            quantise_w1(a, 1, round_w1(a, 1, nc.scalar.copy if a == 1 else nc.vector.tensor_copy))
+            first_product(a, 1, 0)
+        energies(1, 0)
+        quantise_z(1, 0)
+        for a in range(KA):
+            first_product(a, 1, 1)
+        for c in range(NC):
+            gather_readings(c)
+        last, before = NC - 1, NC - 2
+        second_product(last, 0, 0)
+        scatter(last, 0, 1)
+        quantise_z(0, 1)
+        energies(1, 1)
+        quantise_z(1, 1)
+        second_product(before, 0, 7)
+        scatter(before, 0, 1)
+        for i, c in enumerate((last, before)):
+            second_product(c, 1, 1 + i)
+            scatter(c, 1, 1)
+            store(c)
+        for c in range(NC - 2):
+            for h in range(HALVES):
+                second_product(c, h, (2 * c + h + 3) % 8)
+            scatter(c, 0, HALVES)
+            store(c)

@@ -41,16 +41,21 @@ def tile_list_jaw_scatter_correction_kernel(
             return psum.tile([P, HALF], F32, name="bank%d" % i)
 
         offsets = keep.tile([P, S // 16], U16, name="offsets")
-        nc.sync.dma_start(offsets[:], offs)
 
         tab_plane = keep.tile([P, T], U8, name="tab_plane", tag="tab_plane", align_bytes=64)
         nc.gpsimd.memset(tab_plane[:].bitcast(I32), 0)
+        for q in range(4):
+            nc.gpsimd.dma_start(
+                tab_plane[32 * q : 32 * q + 4 * KA, :].bitcast(I32),
+                tab_scales[:, 4 * q : 4 * q + 4, :].bitcast(I32),
+            )
         w4_plane = keep.tile([P, HB * N], U8, name="w4_plane", align_bytes=64)
         nc.vector.memset(w4_plane[:].bitcast(I32), 0)
         air_rows = keep.tile([P, P], F32, name="air_rows")
         nc.gpsimd.memset(air_rows[:], 0.0)
 
         gain_cols = keep.tile([P, HB, PACK], F32, name="gain_cols")
+        nc.scalar.dma_start(gain_cols[:], gain.rearrange("(b p t) -> p b t", b=HB, t=PACK))
         nc.gpsimd.dma_start(air_rows[0:NC, :], air.rearrange("(c p) -> c p", p=P))
 
         w_raw, tab = {}, {}
@@ -59,11 +64,7 @@ def tile_list_jaw_scatter_correction_kernel(
             raw = keep.tile([P, PACK, KP], F32, name="w_raw%d%d" % (a, b))
             rows = w1[a * KP : (a + 1) * KP, b * KP : (b + 1) * KP]
             rows = rows.rearrange("(p j) c -> p j c", j=PACK)
-            if (a, b) == (0, 0):
-                nc.sync.dma_start(raw[:, 0:2, :], rows[:, 0:2, :])
-                nc.sync.dma_start(raw[:, 2:4, :], rows[:, 2:4, :])
-            else:
-                nc.sync.dma_start(raw[:], rows)
+            nc.sync.dma_start(raw[:], rows)
             w_raw[a, b] = raw
 
         def load_tab(a):
@@ -74,13 +75,8 @@ def tile_list_jaw_scatter_correction_kernel(
             tab[a] = words
 
         load_tab(0)
-        nc.sync.dma_start(gain_cols[:], gain.rearrange("(b p t) -> p b t", b=HB, t=PACK))
+        nc.sync.dma_start(offsets[:], offs)
         load_w1(0, 0)
-        for q in range(4):
-            nc.sync.dma_start(
-                tab_plane[32 * q : 32 * q + 4 * KA, :].bitcast(I32),
-                tab_scales[:, 4 * q : 4 * q + 4, :].bitcast(I32),
-            )
         load_tab(1)
         load_w1(1, 0)
         load_w1(2, 0)
@@ -89,16 +85,25 @@ def tile_list_jaw_scatter_correction_kernel(
             load_w1(a, 1)
 
         readings = []
-        w4_codes = keep.tile([P, HB * 2 * N], U8, name="w4_codes", align_bytes=64)
+        w4_codes = {}
+
+        def load_w4(first, end):
+            codes = keep.tile([P, HB, 2 * P * (end - first)], U8, name="w4_codes%d" % first, align_bytes=64)
+            nc.sync.dma_start(
+                codes[:].bitcast(I32),
+                w4_words[:, :, 2 * P * first : 2 * P * end].bitcast(I32).rearrange("b p w -> p b w"),
+            )
+            for c in range(first, end):
+                w4_codes[c] = codes[:, :, 2 * P * (c - first) : 2 * P * (c - first + 1)]
+
         for c in range(NC):
             rows = keep.tile([P, T], F32, name="readings%d" % c)
             nc.sync.dma_start(rows[:], gT[c * P : (c + 1) * P, :])
             readings.append(rows)
             if c == NC - 1:
-                nc.sync.dma_start(
-                    w4_codes[:].bitcast(I32).rearrange("p (b w) -> p b w", b=HB),
-                    w4_words.bitcast(I32).rearrange("b p w -> p b w"),
-                )
+                load_w4(0, NC - 2)
+            if c == 2:
+                load_w4(NC - 2, NC)
                 for q in range(4):
                     nc.sync.dma_start(
                         w4_plane[32 * q : 32 * q + 4, :].bitcast(I32).rearrange("r (b w) -> r b w", b=HB),
@@ -198,7 +203,7 @@ def tile_list_jaw_scatter_correction_kernel(
             for b in range(HB):
                 nc.tensor.matmul_mx(
                     out=y_bank[:],
-                    lhsT=w4_codes[:, 2 * (b * N + c * P) : 2 * (b * N + (c + 1) * P)].bitcast(FP4X4),
+                    lhsT=w4_codes[c][:, b, :].bitcast(FP4X4),
                     lhsT_scale=w4_plane[:, b * N + c * P : b * N + (c + 1) * P],
                     rhs=z_codes[b, h][:].bitcast(FP8X4),
                     rhs_scale=z_plane[b, h][:],

@@ -19,13 +19,22 @@ MULT = mybir.AluOpType.mult
 
 P = 128
 PACK = 4
-KP = P * PACK
-KA = K // KP
-HB = H // KP
-NC = N // P
+PASS = P * PACK
+PASSES = K // PASS
+BLOCKS = H // PASS
+VIEW_TILES = N // P
 HALF = 512
 HALVES = S // HALF
-LIST_COLS = HALF // 16
+LIST_GROUP = 16
+QUADRANTS = 4
+QUADRANT = P // QUADRANTS
+PLANE_ROWS = 4
+FP4_BYTES = 2
+BANKS = 8
+RUN = 4
+INVERSE_TILES = 4
+W4_AFTER = 2
+SPLIT_TILES = (5, 4, 3)
 
 
 def tile_list_jaw_scatter_correction_kernel(
@@ -37,35 +46,31 @@ def tile_list_jaw_scatter_correction_kernel(
         ring = ctx.enter_context(tc.tile_pool(name="ring", bufs=2))
         psum = ctx.enter_context(tc.psum_pool(name="psum", bufs=1))
 
-        def bank(i):
-            return psum.tile([P, HALF], F32, name="bank%d" % i)
+        def bank(number):
+            return psum.tile([P, HALF], F32, name="bank%d" % number)
 
-        offsets = keep.tile([P, S // 16], U16, name="offsets")
+        offsets = keep.tile([P, S // LIST_GROUP], U16, name="offsets")
+        nc.sync.dma_start(offsets[:], offs)
 
         tab_plane = keep.tile([P, T], U8, name="tab_plane", tag="tab_plane", align_bytes=64)
         nc.gpsimd.memset(tab_plane[:].bitcast(I32), 0)
-        for q in range(4):
-            nc.gpsimd.dma_start(
-                tab_plane[32 * q : 32 * q + 4 * KA, :].bitcast(I32),
-                tab_scales[:, 4 * q : 4 * q + 4, :].bitcast(I32),
-            )
-        w4_plane = keep.tile([P, HB * N], U8, name="w4_plane", align_bytes=64)
+        w4_plane = keep.tile([P, BLOCKS * N], U8, name="w4_plane", align_bytes=64)
         nc.vector.memset(w4_plane[:].bitcast(I32), 0)
         air_rows = keep.tile([P, P], F32, name="air_rows")
         nc.gpsimd.memset(air_rows[:], 0.0)
 
-        gain_cols = keep.tile([P, HB, PACK], F32, name="gain_cols")
-        nc.scalar.dma_start(gain_cols[:], gain.rearrange("(b p t) -> p b t", b=HB, t=PACK))
-        nc.gpsimd.dma_start(air_rows[0:NC, :], air.rearrange("(c p) -> c p", p=P))
+        gain_cols = keep.tile([P, BLOCKS, PACK], F32, name="gain_cols")
+        nc.gpsimd.dma_start(air_rows[0:VIEW_TILES, :], air.rearrange("(c p) -> c p", p=P))
 
         w_raw, tab = {}, {}
 
-        def load_w1(a, b):
-            raw = keep.tile([P, PACK, KP], F32, name="w_raw%d%d" % (a, b))
-            rows = w1[a * KP : (a + 1) * KP, b * KP : (b + 1) * KP]
-            rows = rows.rearrange("(p j) c -> p j c", j=PACK)
-            nc.sync.dma_start(raw[:], rows)
-            w_raw[a, b] = raw
+        def load_w1(a, blocks):
+            cols = slice(blocks[0] * PASS, (blocks[-1] + 1) * PASS)
+            raw = keep.tile([P, PACK, len(blocks) * PASS], F32, name="w_raw%d%d" % (a, blocks[0]))
+            rows = w1[a * PASS : (a + 1) * PASS, cols]
+            nc.sync.dma_start(raw[:], rows.rearrange("(p j) c -> p j c", j=PACK))
+            for i, b in enumerate(blocks):
+                w_raw[a, b] = raw[:, :, i * PASS : (i + 1) * PASS]
 
         def load_tab(a):
             words = keep.tile([P, T], U32, name="tab%d" % a, align_bytes=64)
@@ -75,119 +80,110 @@ def tile_list_jaw_scatter_correction_kernel(
             tab[a] = words
 
         load_tab(0)
-        nc.sync.dma_start(offsets[:], offs)
-        load_w1(0, 0)
+        nc.sync.dma_start(gain_cols[:], gain.rearrange("(b p t) -> p b t", b=BLOCKS, t=PACK))
+        for q in range(QUADRANTS):
+            nc.sync.dma_start(
+                tab_plane[QUADRANT * q : QUADRANT * q + PLANE_ROWS * PASSES, :].bitcast(I32),
+                tab_scales[:, PLANE_ROWS * q : PLANE_ROWS * (q + 1), :].bitcast(I32),
+            )
+        load_w1(0, (0, 1))
         load_tab(1)
-        load_w1(1, 0)
-        load_w1(2, 0)
         load_tab(2)
-        for a in range(KA):
-            load_w1(a, 1)
+        load_w1(1, (0, 1))
+        load_w1(2, (0,))
+        load_w1(2, (1,))
 
         readings = []
-        w4_codes = {}
-
-        def load_w4(first, end):
-            codes = keep.tile([P, HB, 2 * P * (end - first)], U8, name="w4_codes%d" % first, align_bytes=64)
-            nc.sync.dma_start(
-                codes[:].bitcast(I32),
-                w4_words[:, :, 2 * P * first : 2 * P * end].bitcast(I32).rearrange("b p w -> p b w"),
-            )
-            for c in range(first, end):
-                w4_codes[c] = codes[:, :, 2 * P * (c - first) : 2 * P * (c - first + 1)]
-
-        for c in range(NC):
+        w4_codes = keep.tile([P, BLOCKS * FP4_BYTES * N], U8, name="w4_codes", align_bytes=64)
+        for c in range(VIEW_TILES):
             rows = keep.tile([P, T], F32, name="readings%d" % c)
             nc.sync.dma_start(rows[:], gT[c * P : (c + 1) * P, :])
             readings.append(rows)
-            if c == NC - 1:
-                load_w4(0, NC - 2)
-            if c == 2:
-                load_w4(NC - 2, NC)
-                for q in range(4):
+            if c == W4_AFTER:
+                nc.sync.dma_start(
+                    w4_codes[:].bitcast(I32).rearrange("p (b w) -> p b w", b=BLOCKS),
+                    w4_words.bitcast(I32).rearrange("b p w -> p b w"),
+                )
+                for q in range(QUADRANTS):
                     nc.sync.dma_start(
-                        w4_plane[32 * q : 32 * q + 4, :].bitcast(I32).rearrange("r (b w) -> r b w", b=HB),
-                        w4_scales[:, 4 * q : 4 * q + 4, :].bitcast(I32).rearrange("b r w -> r b w"),
+                        w4_plane[QUADRANT * q : QUADRANT * q + PLANE_ROWS, :]
+                        .bitcast(I32)
+                        .rearrange("r (b w) -> r b w", b=BLOCKS),
+                        w4_scales[:, PLANE_ROWS * q : PLANE_ROWS * (q + 1), :]
+                        .bitcast(I32)
+                        .rearrange("b r w -> r b w"),
                     )
 
         gain_flat = gain_cols[:].rearrange("p b t -> p (b t)")
-        gain_rsqrt = keep.tile([P, HB * PACK], F32, name="gain_rsqrt")
+        gain_rsqrt = keep.tile([P, BLOCKS * PACK], F32, name="gain_rsqrt")
         nc.scalar.activation(gain_rsqrt[:], gain_flat, ACT.Abs_reciprocal_sqrt)
-        gain_root = keep.tile([P, HB * PACK], F32, name="gain_root")
+        gain_root = keep.tile([P, BLOCKS * PACK], F32, name="gain_root")
         nc.gpsimd.tensor_tensor(gain_root[:], gain_flat, gain_rsqrt[:], MULT)
 
         identity = keep.tile([P, P], F32, name="identity")
         make_identity(nc, identity[:])
-        air_cols = keep.tile([P, NC], F32, name="air_cols")
+        air_cols = keep.tile([P, VIEW_TILES], F32, name="air_cols")
 
         v_plane = keep.tile([P, S], U8, name="v_plane", align_bytes=64)
         nc.vector.tensor_copy(v_plane[:], tab_plane[:].indirect(offsets[:]))
 
         w_codes, w_plane, v_words = {}, {}, {}
 
-        def round_w1(a, b, copy):
-            rounded = ring.tile([P, PACK * KP], BF16, name="w_rounded", align_bytes=64)
+        def quantise_w1(a, b, copy):
+            rounded = ring.tile([P, PACK * PASS], BF16, name="w_rounded", align_bytes=64)
             copy(
                 rounded[:].rearrange("p (t m j) -> p m j t", t=PACK, j=PACK),
-                w_raw[a, b][:].rearrange("p j (m t) -> p m j t", t=PACK),
+                w_raw[a, b].rearrange("p j (m t) -> p m j t", t=PACK),
             )
-            return rounded
-
-        def quantise_w1(a, b, rounded):
-            codes = keep.tile([P, KP], U32, name="w_codes%d%d" % (a, b), align_bytes=64)
+            codes = keep.tile([P, PASS], U32, name="w_codes%d%d" % (a, b), align_bytes=64)
             tag = "tab_plane" if (a, b) == (0, 0) else "w_plane%d%d" % (a, b)
-            plane = keep.tile([P, KP], U8, name="w_plane%d%d" % (a, b), tag=tag, align_bytes=64)
+            plane = keep.tile([P, PASS], U8, name="w_plane%d%d" % (a, b), tag=tag, align_bytes=64)
             nc.vector.quantize_mx(out=codes[:].bitcast(FP8X4), scales=plane[:], in_=rounded[:])
             w_codes[a, b], w_plane[a, b] = codes, plane
 
-        def gather_words(a, pieces):
+        def gather_words(a):
             words = keep.tile([P, S], U32, name="v_words%d" % a, align_bytes=64)
-            width = S // pieces
-            for i in range(pieces):
-                nc.vector.tensor_copy(
-                    words[:, i * width : (i + 1) * width],
-                    tab[a][:].indirect(offsets[:, i * width // 16 : (i + 1) * width // 16]),
-                )
+            nc.vector.tensor_copy(words[:], tab[a][:].indirect(offsets[:]))
             v_words[a] = words
 
         h_banks = {}
 
-        def first_product(a, b, h):
-            cols = slice(h * HALF, (h + 1) * HALF)
+        def first_product(a, b, half):
+            cols = slice(half * HALF, (half + 1) * HALF)
             for t in range(PACK):
                 if a == 0:
-                    h_banks[b, h, t] = bank(PACK * h + t)
+                    h_banks[b, half, t] = bank(PACK * b + t)
                 nc.tensor.matmul_mx(
-                    out=h_banks[b, h, t][:],
+                    out=h_banks[b, half, t][:],
                     lhsT=w_codes[a, b][:, t * P : (t + 1) * P].bitcast(FP8X4),
                     lhsT_scale=w_plane[a, b][:, t * P : (t + 1) * P],
                     rhs=v_words[a][:, cols].bitcast(FP8X4),
-                    rhs_scale=v_plane[4 * a : P, cols],
+                    rhs_scale=v_plane[PLANE_ROWS * a : P, cols],
                     start=(a == 0),
-                    stop=(a == KA - 1),
+                    stop=(a == PASSES - 1),
                 )
 
         z_rows, z_codes, z_plane = {}, {}, {}
 
-        def energies(b, h):
+        def energies(b, half):
             rows = ring.tile([P, PACK, HALF], BF16, name="z_rows")
             for t in range(PACK):
                 col = PACK * b + t
                 nc.scalar.activation(
-                    rows[:, t, :], h_banks[b, h, t][:], ACT.Square, scale=gain_root[:, col : col + 1]
+                    rows[:, t, :], h_banks[b, half, t][:], ACT.Square, scale=gain_root[:, col : col + 1]
                 )
-            z_rows[b, h] = rows
+            z_rows[b, half] = rows
 
-        def quantise_z(b, h):
+        def quantise_z(b, half):
             woven = ring.tile([P, PACK * HALF], BF16, name="z_woven", align_bytes=64)
             nc.scalar.copy(
-                woven[:].rearrange("p (c i t) -> p c t i", i=4, t=PACK),
-                z_rows[b, h][:].rearrange("p t (c i) -> p c t i", i=4),
+                woven[:].rearrange("p (c i t) -> p c t i", i=RUN, t=PACK),
+                z_rows[b, half][:].rearrange("p t (c i) -> p c t i", i=RUN),
             )
-            codes = keep.tile([P, HALF], U32, name="z_codes%d%d" % (b, h), align_bytes=64)
-            plane = keep.tile([P, HALF], U8, name="z_plane%d%d" % (b, h), align_bytes=64)
+            codes = keep.tile([P, HALF], U32, name="z_codes%d%d" % (b, half), align_bytes=64)
+            plane = keep.tile([P, HALF], U8, name="z_plane%d%d" % (b, half), align_bytes=64)
             nc.vector.quantize_mx(out=codes[:].bitcast(FP8X4), scales=plane[:], in_=woven[:])
-            z_codes[b, h], z_plane[b, h] = codes, plane
+            z_codes[b, half], z_plane[b, half] = codes, plane
 
         picked = {}
 
@@ -198,70 +194,79 @@ def tile_list_jaw_scatter_correction_kernel(
 
         inverse = {}
 
-        def second_product(c, h, i):
-            y_bank = bank(i)
-            for b in range(HB):
+        def second_product(c, half, number):
+            y_bank = bank(number)
+            for b in range(BLOCKS):
+                first = b * N + c * P
                 nc.tensor.matmul_mx(
                     out=y_bank[:],
-                    lhsT=w4_codes[c][:, b, :].bitcast(FP4X4),
-                    lhsT_scale=w4_plane[:, b * N + c * P : b * N + (c + 1) * P],
-                    rhs=z_codes[b, h][:].bitcast(FP8X4),
-                    rhs_scale=z_plane[b, h][:],
+                    lhsT=w4_codes[:, FP4_BYTES * first : FP4_BYTES * (first + P)].bitcast(FP4X4),
+                    lhsT_scale=w4_plane[:, first : first + P],
+                    rhs=z_codes[b, half][:].bitcast(FP8X4),
+                    rhs_scale=z_plane[b, half][:],
                     start=(b == 0),
-                    stop=(b == HB - 1),
+                    stop=(b == BLOCKS - 1),
                 )
             root = ring.tile([P, HALF], F32, name="root")
             nc.scalar.activation(root[:], y_bank[:], ACT.Abs_reciprocal_sqrt, bias=air_cols[:, c : c + 1])
-            if h == 0:
-                inverse[c] = ring.tile([P, S], F32, name="inverse", bufs=4)
-            nc.scalar.activation(inverse[c][:, h * HALF : (h + 1) * HALF], root[:], ACT.Square)
+            if half == 0:
+                inverse[c] = ring.tile([P, S], F32, name="inverse", bufs=INVERSE_TILES)
+            nc.scalar.activation(inverse[c][:, half * HALF : (half + 1) * HALF], root[:], ACT.Square)
 
-        def scatter(c, first, count):
-            cols = slice(first * HALF, (first + count) * HALF)
+        def scatter(c, halves):
+            start, stop = halves.start * HALF, halves.stop * HALF
             nc.vector.tensor_tensor(
-                readings[c][:].indirect(offsets[:, first * LIST_COLS : (first + count) * LIST_COLS]),
-                picked[c][:, cols],
-                inverse[c][:, cols],
+                readings[c][:].indirect(offsets[:, start // LIST_GROUP : stop // LIST_GROUP]),
+                picked[c][:, start:stop],
+                inverse[c][:, start:stop],
                 MULT,
             )
 
         def store(c):
             nc.sync.dma_start(out[c * P : (c + 1) * P, :], readings[c][:])
 
-        for a in range(KA):
-            quantise_w1(a, 0, round_w1(a, 0, nc.vector.tensor_copy if a == 1 else nc.scalar.copy))
-            gather_words(a, 2 if a == KA - 1 else 1)
-            for h in range(HALVES):
-                first_product(a, 0, h)
-        energies(0, 0)
-        quantise_z(0, 0)
-        energies(0, 1)
-        air_bank = bank(PACK)
-        nc.tensor.transpose(air_bank[:, 0:P], air_rows[:], identity[:])
-        nc.scalar.copy(air_cols[:], air_bank[:, 0:NC])
-        for a in range(KA):
-            quantise_w1(a, 1, round_w1(a, 1, nc.scalar.copy if a == 1 else nc.vector.tensor_copy))
+        for a in range(PASSES):
+            gather_words(a)
+            quantise_w1(a, 0, nc.scalar.copy if a == 0 else nc.vector.tensor_copy)
+            first_product(a, 0, 0)
+            if a == PASSES - 1:
+                energies(0, 0)
+                quantise_z(0, 0)
+            quantise_w1(a, 1, nc.vector.tensor_copy if a == PASSES - 1 else nc.scalar.copy)
             first_product(a, 1, 0)
         energies(1, 0)
         quantise_z(1, 0)
-        for a in range(KA):
-            first_product(a, 1, 1)
-        for c in range(NC):
+
+        air_bank = bank(PACK - 1)
+        nc.tensor.transpose(air_bank[:, 0:P], air_rows[:], identity[:])
+        nc.scalar.copy(air_cols[:], air_bank[:, 0:VIEW_TILES])
+
+        for a in range(PASSES):
+            first_product(a, 0, 1)
+        for c in range(VIEW_TILES):
             gather_readings(c)
-        last, before = NC - 1, NC - 2
-        second_product(last, 0, 0)
-        scatter(last, 0, 1)
+        energies(0, 1)
+        for a in range(PASSES):
+            first_product(a, 1, 1)
+
+        for i, c in enumerate(SPLIT_TILES[:-1]):
+            second_product(c, 0, i)
+            scatter(c, range(0, 1))
         quantise_z(0, 1)
         energies(1, 1)
         quantise_z(1, 1)
-        second_product(before, 0, 7)
-        scatter(before, 0, 1)
-        for i, c in enumerate((last, before)):
-            second_product(c, 1, 1 + i)
-            scatter(c, 1, 1)
+        second_product(SPLIT_TILES[-1], 0, BANKS - 1)
+        scatter(SPLIT_TILES[-1], range(0, 1))
+
+        next_bank = len(SPLIT_TILES) - 1
+        for c in SPLIT_TILES:
+            second_product(c, 1, next_bank % BANKS)
+            next_bank = next_bank + 1
+            scatter(c, range(1, HALVES))
             store(c)
-        for c in range(NC - 2):
-            for h in range(HALVES):
-                second_product(c, h, (2 * c + h + 3) % 8)
-            scatter(c, 0, HALVES)
+        for c in range(VIEW_TILES - len(SPLIT_TILES)):
+            for half in range(HALVES):
+                second_product(c, half, next_bank % BANKS)
+                next_bank = next_bank + 1
+            scatter(c, range(0, HALVES))
             store(c)

@@ -56,54 +56,68 @@ def tile_list_jaw_scatter_correction_kernel(
         nc.gpsimd.memset(tab_plane[:].bitcast(I32), 0)
         w4_plane = keep.tile([P, BLOCKS * N], U8, name="w4_plane", align_bytes=64)
         nc.vector.memset(w4_plane[:].bitcast(I32), 0)
-        air_rows = keep.tile([P, P], F32, name="air_rows")
+        air_rows = keep.tile([P, P], F32, name="air_rows", tag="air_rows", align_bytes=64)
         nc.gpsimd.memset(air_rows[:], 0.0)
+        gain_rows = keep.tile([P, PASS], F32, name="gain_rows")
+        nc.vector.memset(gain_rows[:], 0.0)
 
-        gain_cols = keep.tile([P, BLOCKS, PACK], F32, name="gain_cols")
-        nc.gpsimd.dma_start(air_rows[0:VIEW_TILES, :], air.rearrange("(c p) -> c p", p=P))
+        nc.scalar.dma_start(gain_rows[0:BLOCKS, :], gain.rearrange("(b r) -> b r", b=BLOCKS))
 
         w_raw, tab = {}, {}
 
         def load_w1(a, blocks):
             cols = slice(blocks[0] * PASS, (blocks[-1] + 1) * PASS)
-            raw = keep.tile([P, PACK, len(blocks) * PASS], F32, name="w_raw%d%d" % (a, blocks[0]))
+            name = "w_raw%d%d" % (a, blocks[0])
+            raw = keep.tile([P, PACK, len(blocks) * PASS], F32, name=name, tag=name, align_bytes=64)
             rows = w1[a * PASS : (a + 1) * PASS, cols]
             nc.sync.dma_start(raw[:], rows.rearrange("(p j) c -> p j c", j=PACK))
             for i, b in enumerate(blocks):
                 w_raw[a, b] = raw[:, :, i * PASS : (i + 1) * PASS]
 
         def load_tab(a):
-            words = keep.tile([P, T], U32, name="tab%d" % a, align_bytes=64)
+            words = keep.tile([P, T], U32, name="tab%d" % a, tag="tab%d" % a, align_bytes=64)
             nc.sync.dma_start(
                 words[:].bitcast(I32), tab_words[a].rearrange("p n i -> p (n i)").bitcast(I32)
             )
             tab[a] = words
 
-        load_tab(0)
-        nc.sync.dma_start(gain_cols[:], gain.rearrange("(b p t) -> p b t", b=BLOCKS, t=PACK))
+        for a in range(PASSES):
+            load_tab(a)
         for q in range(QUADRANTS):
             nc.sync.dma_start(
                 tab_plane[QUADRANT * q : QUADRANT * q + PLANE_ROWS * PASSES, :].bitcast(I32),
                 tab_scales[:, PLANE_ROWS * q : PLANE_ROWS * (q + 1), :].bitcast(I32),
             )
         load_w1(0, (0, 1))
-        load_tab(1)
-        load_tab(2)
         load_w1(1, (0, 1))
         load_w1(2, (0,))
         load_w1(2, (1,))
 
         readings = []
-        w4_codes = keep.tile([P, BLOCKS * FP4_BYTES * N], U8, name="w4_codes", align_bytes=64)
+        w4_codes = {}
+
+        def load_w4(tiles):
+            width = len(tiles) * FP4_BYTES * P
+            codes = keep.tile([P, BLOCKS * width], U8, name="w4_codes%d" % tiles.start, align_bytes=64)
+            start = tiles.start * FP4_BYTES * P
+            nc.sync.dma_start(
+                codes[:].bitcast(I32).rearrange("p (b w) -> p b w", b=BLOCKS),
+                w4_words[:, :, start : start + width].bitcast(I32).rearrange("b p w -> p b w"),
+            )
+            for b in range(BLOCKS):
+                for i, c in enumerate(tiles):
+                    first = b * width + i * FP4_BYTES * P
+                    w4_codes[b, c] = codes[:, first : first + FP4_BYTES * P]
+
         for c in range(VIEW_TILES):
             rows = keep.tile([P, T], F32, name="readings%d" % c)
             nc.sync.dma_start(rows[:], gT[c * P : (c + 1) * P, :])
             readings.append(rows)
-            if c == W4_AFTER:
-                nc.sync.dma_start(
-                    w4_codes[:].bitcast(I32).rearrange("p (b w) -> p b w", b=BLOCKS),
-                    w4_words.bitcast(I32).rearrange("b p w -> p b w"),
-                )
+            if c == VIEW_TILES - 1:
+                load_w4(range(0, VIEW_TILES - 1))
+            if c == W4_AFTER + 1:
+                nc.sync.dma_start(air_rows[0:VIEW_TILES, :], air.rearrange("(c p) -> c p", p=P))
+                load_w4(range(VIEW_TILES - 1, VIEW_TILES))
                 for q in range(QUADRANTS):
                     nc.sync.dma_start(
                         w4_plane[QUADRANT * q : QUADRANT * q + PLANE_ROWS, :]
@@ -114,23 +128,25 @@ def tile_list_jaw_scatter_correction_kernel(
                         .rearrange("b r w -> r b w"),
                     )
 
+        identity = keep.tile([P, P], F32, name="identity")
+        make_identity(nc, identity[:])
+        gain_bank = bank(BANKS - 1)
+        for t in range(PACK):
+            nc.tensor.transpose(gain_bank[:, t * P : (t + 1) * P], gain_rows[:, t:PASS:PACK], identity[:])
+        gain_cols = keep.tile([P, BLOCKS, PACK], F32, name="gain_cols")
+        nc.scalar.copy(gain_cols[:], gain_bank[:].rearrange("p (t b) -> p b t", t=PACK)[:, 0:BLOCKS, :])
         gain_flat = gain_cols[:].rearrange("p b t -> p (b t)")
         gain_rsqrt = keep.tile([P, BLOCKS * PACK], F32, name="gain_rsqrt")
         nc.scalar.activation(gain_rsqrt[:], gain_flat, ACT.Abs_reciprocal_sqrt)
         gain_root = keep.tile([P, BLOCKS * PACK], F32, name="gain_root")
         nc.gpsimd.tensor_tensor(gain_root[:], gain_flat, gain_rsqrt[:], MULT)
 
-        identity = keep.tile([P, P], F32, name="identity")
-        make_identity(nc, identity[:])
         air_cols = keep.tile([P, VIEW_TILES], F32, name="air_cols")
-
-        v_plane = keep.tile([P, S], U8, name="v_plane", align_bytes=64)
-        nc.vector.tensor_copy(v_plane[:], tab_plane[:].indirect(offsets[:]))
 
         w_codes, w_plane, v_words = {}, {}, {}
 
         def quantise_w1(a, b, copy):
-            rounded = ring.tile([P, PACK * PASS], BF16, name="w_rounded", align_bytes=64)
+            rounded = ring.tile([P, PACK * PASS], BF16, name="w_rounded", bufs=3, align_bytes=64)
             copy(
                 rounded[:].rearrange("p (t m j) -> p m j t", t=PACK, j=PACK),
                 w_raw[a, b].rearrange("p j (m t) -> p m j t", t=PACK),
@@ -145,6 +161,11 @@ def tile_list_jaw_scatter_correction_kernel(
             words = keep.tile([P, S], U32, name="v_words%d" % a, align_bytes=64)
             nc.vector.tensor_copy(words[:], tab[a][:].indirect(offsets[:]))
             v_words[a] = words
+
+        for a in range(PASSES):
+            gather_words(a)
+        v_plane = keep.tile([P, S], U8, name="v_plane", align_bytes=64)
+        nc.vector.tensor_copy(v_plane[:], tab_plane[:].indirect(offsets[:]))
 
         h_banks = {}
 
@@ -163,10 +184,13 @@ def tile_list_jaw_scatter_correction_kernel(
                     stop=(a == PASSES - 1),
                 )
 
-        z_rows, z_codes, z_plane = {}, {}, {}
+        z_rows, z_woven, z_codes, z_plane = {}, {}, {}, {}
 
         def energies(b, half):
-            rows = ring.tile([P, PACK, HALF], BF16, name="z_rows")
+            if (b, half) == (BLOCKS - 1, HALVES - 1):
+                rows = keep.tile([P, PACK, HALF], BF16, name="z_rows_last", tag="first_root")
+            else:
+                rows = ring.tile([P, PACK, HALF], BF16, name="z_rows")
             for t in range(PACK):
                 col = PACK * b + t
                 nc.scalar.activation(
@@ -174,21 +198,28 @@ def tile_list_jaw_scatter_correction_kernel(
                 )
             z_rows[b, half] = rows
 
-        def quantise_z(b, half):
-            woven = ring.tile([P, PACK * HALF], BF16, name="z_woven", align_bytes=64)
+        def weave_z(b, half):
+            if b == 0:
+                z_woven[half] = ring.tile([P, BLOCKS * PACK * HALF], BF16, name="z_woven", align_bytes=64)
             nc.scalar.copy(
-                woven[:].rearrange("p (c i t) -> p c t i", i=RUN, t=PACK),
+                z_woven[half][:, b * PACK * HALF : (b + 1) * PACK * HALF].rearrange(
+                    "p (c i t) -> p c t i", i=RUN, t=PACK
+                ),
                 z_rows[b, half][:].rearrange("p t (c i) -> p c t i", i=RUN),
             )
-            codes = keep.tile([P, HALF], U32, name="z_codes%d%d" % (b, half), align_bytes=64)
-            plane = keep.tile([P, HALF], U8, name="z_plane%d%d" % (b, half), align_bytes=64)
-            nc.vector.quantize_mx(out=codes[:].bitcast(FP8X4), scales=plane[:], in_=woven[:])
-            z_codes[b, half], z_plane[b, half] = codes, plane
+
+        def quantise_z(half):
+            codes = keep.tile([P, BLOCKS * HALF], U32, name="z_codes%d" % half, align_bytes=64)
+            tag = "air_rows" if half == 0 else "first_inverse"
+            plane = keep.tile([P, BLOCKS * HALF], U8, name="z_plane%d" % half, tag=tag, align_bytes=64)
+            nc.vector.quantize_mx(out=codes[:].bitcast(FP8X4), scales=plane[:], in_=z_woven[half][:])
+            z_codes[half], z_plane[half] = codes, plane
 
         picked = {}
 
         def gather_readings(c):
-            values = keep.tile([P, S], F32, name="picked%d" % c)
+            tag = "tab%d" % c if c < PASSES else "w_raw%d0" % (c - PASSES)
+            values = keep.tile([P, S], F32, name="picked%d" % c, tag=tag, align_bytes=64)
             nc.vector.tensor_copy(values[:], readings[c][:].indirect(offsets[:]))
             picked[c] = values
 
@@ -200,25 +231,37 @@ def tile_list_jaw_scatter_correction_kernel(
                 first = b * N + c * P
                 nc.tensor.matmul_mx(
                     out=y_bank[:],
-                    lhsT=w4_codes[:, FP4_BYTES * first : FP4_BYTES * (first + P)].bitcast(FP4X4),
+                    lhsT=w4_codes[b, c].bitcast(FP4X4),
                     lhsT_scale=w4_plane[:, first : first + P],
-                    rhs=z_codes[b, half][:].bitcast(FP8X4),
-                    rhs_scale=z_plane[b, half][:],
+                    rhs=z_codes[half][:, b * HALF : (b + 1) * HALF].bitcast(FP8X4),
+                    rhs_scale=z_plane[half][:, b * HALF : (b + 1) * HALF],
                     start=(b == 0),
                     stop=(b == BLOCKS - 1),
                 )
-            root = ring.tile([P, HALF], F32, name="root")
+            first_of_all = (c, half) == (SPLIT_TILES[0], 0)
+            if (c, half) == (SPLIT_TILES[1], 0):
+                root = keep.tile([P, HALF], F32, name="first_root", tag="first_root")
+            else:
+                root = ring.tile([P, HALF], F32, name="root")
             nc.scalar.activation(root[:], y_bank[:], ACT.Abs_reciprocal_sqrt, bias=air_cols[:, c : c + 1])
-            if half == 0:
-                inverse[c] = ring.tile([P, S], F32, name="inverse", bufs=INVERSE_TILES)
-            nc.scalar.activation(inverse[c][:, half * HALF : (half + 1) * HALF], root[:], ACT.Square)
+            if first_of_all:
+                whole = keep.tile([P, HALF], F32, name="first_inverse", tag="first_inverse", align_bytes=64)
+                inverse[c, half] = whole[:]
+            elif c in SPLIT_TILES:
+                whole = ring.tile([P, HALF], F32, name="inverse_half", bufs=INVERSE_TILES)
+                inverse[c, half] = whole[:]
+            elif half == 0:
+                whole = ring.tile([P, S], F32, name="inverse")
+                inverse[c] = whole[:]
+                inverse[c, 0], inverse[c, 1] = whole[:, 0:HALF], whole[:, HALF:S]
+            nc.scalar.activation(inverse[c, half], root[:], ACT.Square)
 
         def scatter(c, halves):
             start, stop = halves.start * HALF, halves.stop * HALF
             nc.vector.tensor_tensor(
                 readings[c][:].indirect(offsets[:, start // LIST_GROUP : stop // LIST_GROUP]),
                 picked[c][:, start:stop],
-                inverse[c][:, start:stop],
+                inverse[c, halves.start] if len(halves) == 1 else inverse[c],
                 MULT,
             )
 
@@ -226,39 +269,40 @@ def tile_list_jaw_scatter_correction_kernel(
             nc.sync.dma_start(out[c * P : (c + 1) * P, :], readings[c][:])
 
         for a in range(PASSES):
-            gather_words(a)
-            quantise_w1(a, 0, nc.scalar.copy if a == 0 else nc.vector.tensor_copy)
+            quantise_w1(a, 0, nc.vector.tensor_copy if a == PASSES - 1 else nc.scalar.copy)
             first_product(a, 0, 0)
             if a == PASSES - 1:
                 energies(0, 0)
-                quantise_z(0, 0)
-            quantise_w1(a, 1, nc.vector.tensor_copy if a == PASSES - 1 else nc.scalar.copy)
+                weave_z(0, 0)
+            quantise_w1(a, 1, nc.vector.tensor_copy)
             first_product(a, 1, 0)
         energies(1, 0)
-        quantise_z(1, 0)
+        weave_z(1, 0)
 
-        air_bank = bank(PACK - 1)
+        air_bank = bank(BANKS - 1)
         nc.tensor.transpose(air_bank[:, 0:P], air_rows[:], identity[:])
         nc.scalar.copy(air_cols[:], air_bank[:, 0:VIEW_TILES])
+        quantise_z(0)
 
         for a in range(PASSES):
             first_product(a, 0, 1)
         for c in range(VIEW_TILES):
             gather_readings(c)
         energies(0, 1)
-        for a in range(PASSES):
-            first_product(a, 1, 1)
 
         for i, c in enumerate(SPLIT_TILES[:-1]):
-            second_product(c, 0, i)
+            second_product(c, 0, (0, BANKS - 1)[i])
             scatter(c, range(0, 1))
-        quantise_z(0, 1)
+        for a in range(PASSES):
+            first_product(a, 1, 1)
+        weave_z(0, 1)
         energies(1, 1)
-        quantise_z(1, 1)
+        weave_z(1, 1)
+        quantise_z(1)
         second_product(SPLIT_TILES[-1], 0, BANKS - 1)
         scatter(SPLIT_TILES[-1], range(0, 1))
 
-        next_bank = len(SPLIT_TILES) - 1
+        next_bank = 1
         for c in SPLIT_TILES:
             second_product(c, 1, next_bank % BANKS)
             next_bank = next_bank + 1

@@ -31,10 +31,11 @@ QUADRANT = P // QUADRANTS
 PLANE_ROWS = 4
 FP4_BYTES = 2
 BANKS = 8
+VECTOR_GROUPS = 80
 RUN = 4
 INVERSE_TILES = 4
 W4_AFTER = 2
-SPLIT_TILES = (5, 4, 3)
+SPLIT_TILES = (4, 5, 3)
 
 
 def tile_list_jaw_scatter_correction_kernel(
@@ -114,10 +115,10 @@ def tile_list_jaw_scatter_correction_kernel(
             nc.sync.dma_start(rows[:], gT[c * P : (c + 1) * P, :])
             readings.append(rows)
             if c == VIEW_TILES - 1:
-                load_w4(range(0, VIEW_TILES - 1))
+                load_w4(range(4, VIEW_TILES))
+                load_w4(range(0, 4))
             if c == W4_AFTER + 1:
                 nc.sync.dma_start(air_rows[0:VIEW_TILES, :], air.rearrange("(c p) -> c p", p=P))
-                load_w4(range(VIEW_TILES - 1, VIEW_TILES))
                 for q in range(QUADRANTS):
                     nc.sync.dma_start(
                         w4_plane[QUADRANT * q : QUADRANT * q + PLANE_ROWS, :]
@@ -145,12 +146,13 @@ def tile_list_jaw_scatter_correction_kernel(
 
         w_codes, w_plane, v_words = {}, {}, {}
 
-        def quantise_w1(a, b, copy):
+        def quantise_w1(a, b, shares):
             rounded = ring.tile([P, PACK * PASS], BF16, name="w_rounded", bufs=3, align_bytes=64)
-            copy(
-                rounded[:].rearrange("p (t m j) -> p m j t", t=PACK, j=PACK),
-                w_raw[a, b].rearrange("p j (m t) -> p m j t", t=PACK),
-            )
+            for copy, groups in shares:
+                copy(
+                    rounded[:].rearrange("p (t m j) -> p m j t", t=PACK, j=PACK)[:, groups],
+                    w_raw[a, b].rearrange("p j (m t) -> p m j t", t=PACK)[:, groups],
+                )
             codes = keep.tile([P, PASS], U32, name="w_codes%d%d" % (a, b), align_bytes=64)
             tag = "tab_plane" if (a, b) == (0, 0) else "w_plane%d%d" % (a, b)
             plane = keep.tile([P, PASS], U8, name="w_plane%d%d" % (a, b), tag=tag, align_bytes=64)
@@ -239,7 +241,7 @@ def tile_list_jaw_scatter_correction_kernel(
                     stop=(b == BLOCKS - 1),
                 )
             first_of_all = (c, half) == (SPLIT_TILES[0], 0)
-            if (c, half) == (SPLIT_TILES[1], 0):
+            if half == 0 and c in SPLIT_TILES[:2]:
                 root = keep.tile([P, HALF], F32, name="first_root", tag="first_root")
             else:
                 root = ring.tile([P, HALF], F32, name="root")
@@ -268,13 +270,16 @@ def tile_list_jaw_scatter_correction_kernel(
         def store(c):
             nc.sync.dma_start(out[c * P : (c + 1) * P, :], readings[c][:])
 
+        on_scalar = [(nc.scalar.copy, slice(0, P))]
+        on_vector = [(nc.vector.tensor_copy, slice(0, P))]
+        shared = [(nc.vector.tensor_copy, slice(0, VECTOR_GROUPS)), (nc.scalar.copy, slice(VECTOR_GROUPS, P))]
         for a in range(PASSES):
-            quantise_w1(a, 0, nc.vector.tensor_copy if a == PASSES - 1 else nc.scalar.copy)
+            quantise_w1(a, 0, shared if a == PASSES - 1 else on_scalar)
             first_product(a, 0, 0)
             if a == PASSES - 1:
                 energies(0, 0)
                 weave_z(0, 0)
-            quantise_w1(a, 1, nc.vector.tensor_copy)
+            quantise_w1(a, 1, on_vector)
             first_product(a, 1, 0)
         energies(1, 0)
         weave_z(1, 0)

@@ -53,16 +53,14 @@ def tile_list_jaw_scatter_correction_kernel(
         offsets = keep.tile([P, S // LIST_GROUP], U16, name="offsets")
         nc.sync.dma_start(offsets[:], offs)
 
+        gain_rows = keep.tile([P, PASS], F32, name="gain_rows")
+        nc.vector.memset(gain_rows[:], 0.0)
         tab_plane = keep.tile([P, T], U8, name="tab_plane", tag="tab_plane", align_bytes=64)
         nc.gpsimd.memset(tab_plane[:].bitcast(I32), 0)
         w4_plane = keep.tile([P, BLOCKS * N], U8, name="w4_plane", align_bytes=64)
         nc.vector.memset(w4_plane[:].bitcast(I32), 0)
         air_rows = keep.tile([P, P], F32, name="air_rows", tag="air_rows", align_bytes=64)
         nc.gpsimd.memset(air_rows[:], 0.0)
-        gain_rows = keep.tile([P, PASS], F32, name="gain_rows")
-        nc.vector.memset(gain_rows[:], 0.0)
-
-        nc.scalar.dma_start(gain_rows[0:BLOCKS, :], gain.rearrange("(b r) -> b r", b=BLOCKS))
 
         w_raw, tab = {}, {}
 
@@ -82,15 +80,17 @@ def tile_list_jaw_scatter_correction_kernel(
             )
             tab[a] = words
 
-        for a in range(PASSES):
-            load_tab(a)
+        load_tab(0)
+        nc.sync.dma_start(gain_rows[0:BLOCKS, :], gain.rearrange("(b r) -> b r", b=BLOCKS))
+        load_w1(0, (0, 1))
         for q in range(QUADRANTS):
             nc.sync.dma_start(
                 tab_plane[QUADRANT * q : QUADRANT * q + PLANE_ROWS * PASSES, :].bitcast(I32),
                 tab_scales[:, PLANE_ROWS * q : PLANE_ROWS * (q + 1), :].bitcast(I32),
             )
-        load_w1(0, (0, 1))
         load_w1(1, (0, 1))
+        load_tab(1)
+        load_tab(2)
         load_w1(2, (0,))
         load_w1(2, (1,))
 
@@ -153,7 +153,8 @@ def tile_list_jaw_scatter_correction_kernel(
                     rounded[:].rearrange("p (t m j) -> p m j t", t=PACK, j=PACK)[:, groups],
                     w_raw[a, b].rearrange("p j (m t) -> p m j t", t=PACK)[:, groups],
                 )
-            codes = keep.tile([P, PASS], U32, name="w_codes%d%d" % (a, b), align_bytes=64)
+            tag = "tab%d" % (1 + b) if a == 1 else "w_codes%d%d" % (a, b)
+            codes = keep.tile([P, PASS], U32, name="w_codes%d%d" % (a, b), tag=tag, align_bytes=64)
             tag = "tab_plane" if (a, b) == (0, 0) else "w_plane%d%d" % (a, b)
             plane = keep.tile([P, PASS], U8, name="w_plane%d%d" % (a, b), tag=tag, align_bytes=64)
             nc.vector.quantize_mx(out=codes[:].bitcast(FP8X4), scales=plane[:], in_=rounded[:])
@@ -164,8 +165,7 @@ def tile_list_jaw_scatter_correction_kernel(
             nc.vector.tensor_copy(words[:], tab[a][:].indirect(offsets[:]))
             v_words[a] = words
 
-        for a in range(PASSES):
-            gather_words(a)
+        gather_words(0)
         v_plane = keep.tile([P, S], U8, name="v_plane", align_bytes=64)
         nc.vector.tensor_copy(v_plane[:], tab_plane[:].indirect(offsets[:]))
 
@@ -191,6 +191,8 @@ def tile_list_jaw_scatter_correction_kernel(
         def energies(b, half):
             if (b, half) == (BLOCKS - 1, HALVES - 1):
                 rows = keep.tile([P, PACK, HALF], BF16, name="z_rows_last", tag="first_root")
+            elif (b, half) == (0, 0):
+                rows = keep.tile([P, PACK, HALF], BF16, name="z_rows_first", tag="w_raw21", align_bytes=64)
             else:
                 rows = ring.tile([P, PACK, HALF], BF16, name="z_rows")
             for t in range(PACK):
@@ -220,7 +222,7 @@ def tile_list_jaw_scatter_correction_kernel(
         picked = {}
 
         def gather_readings(c):
-            tag = "tab%d" % c if c < PASSES else "w_raw%d0" % (c - PASSES)
+            tag = ("tab0", "w_raw00", "w_raw10", "w_raw20", "w_raw21", "picked5")[c]
             values = keep.tile([P, S], F32, name="picked%d" % c, tag=tag, align_bytes=64)
             nc.vector.tensor_copy(values[:], readings[c][:].indirect(offsets[:]))
             picked[c] = values
@@ -271,16 +273,17 @@ def tile_list_jaw_scatter_correction_kernel(
             nc.sync.dma_start(out[c * P : (c + 1) * P, :], readings[c][:])
 
         on_scalar = [(nc.scalar.copy, slice(0, P))]
-        on_vector = [(nc.vector.tensor_copy, slice(0, P))]
         shared = [(nc.vector.tensor_copy, slice(0, VECTOR_GROUPS)), (nc.scalar.copy, slice(VECTOR_GROUPS, P))]
         for a in range(PASSES):
-            quantise_w1(a, 0, shared if a == PASSES - 1 else on_scalar)
+            if a == 1:
+                gather_words(1)
+                gather_words(2)
+            quantise_w1(a, 0, on_scalar)
             first_product(a, 0, 0)
-            if a == PASSES - 1:
-                energies(0, 0)
-                weave_z(0, 0)
-            quantise_w1(a, 1, on_vector)
+            quantise_w1(a, 1, shared if a == PASSES - 1 else on_scalar)
             first_product(a, 1, 0)
+        energies(0, 0)
+        weave_z(0, 0)
         energies(1, 0)
         weave_z(1, 0)
 

@@ -31,11 +31,29 @@ QUADRANT = P // QUADRANTS
 PLANE_ROWS = 4
 FP4_BYTES = 2
 BANKS = 8
-VECTOR_GROUPS = 80
+VECTOR_GROUPS = (56, 64)
 RUN = 4
 INVERSE_TILES = 4
 W4_AFTER = 2
-SPLIT_TILES = (4, 5, 3)
+SPLIT_TILES = (5, 4, 3)
+LOAD_ORDER = (0, 1, 2, 3, 5, 4)
+AHEAD = 2
+KIB = 1024
+PLACE = {
+    "picked_late": 0,
+    "z_rows10": 6 * KIB,
+    "z_rows01": 8 * KIB,
+    "w_raw21": 12 * KIB,
+    "z_rows00": 12 * KIB,
+    "picked": 16 * KIB,
+    "tab_plane": 32 * KIB,
+    "w_plane00": 32 * KIB,
+    "w_raw10": 37 * KIB,
+    "v_words2": 37 * KIB,
+    "rounded20": 41 * KIB,
+    "z_rows11": 41 * KIB,
+}
+EARLY_TILES = 4
 
 
 def tile_list_jaw_scatter_correction_kernel(
@@ -45,17 +63,22 @@ def tile_list_jaw_scatter_correction_kernel(
     with ExitStack() as ctx:
         keep = ctx.enter_context(tc.tile_pool(name="keep", bufs=1))
         ring = ctx.enter_context(tc.tile_pool(name="ring", bufs=2))
+        shared = ctx.enter_context(tc.tile_pool(name="shared", bufs=1))
         psum = ctx.enter_context(tc.psum_pool(name="psum", bufs=1))
+
+        def place(shape, dtype, name, tag=None):
+            if name in PLACE:
+                return shared.tile(shape, dtype, name=name, offset=PLACE[name], align_bytes=64)
+            return keep.tile(shape, dtype, name=name, tag=tag or name, align_bytes=64)
 
         def bank(number):
             return psum.tile([P, HALF], F32, name="bank%d" % number)
 
         offsets = keep.tile([P, S // LIST_GROUP], U16, name="offsets")
-        nc.sync.dma_start(offsets[:], offs)
 
         gain_rows = keep.tile([P, PASS], F32, name="gain_rows")
         nc.vector.memset(gain_rows[:], 0.0)
-        tab_plane = keep.tile([P, T], U8, name="tab_plane", tag="tab_plane", align_bytes=64)
+        tab_plane = place([P, T], U8, "tab_plane")
         nc.gpsimd.memset(tab_plane[:].bitcast(I32), 0)
         w4_plane = keep.tile([P, BLOCKS * N], U8, name="w4_plane", align_bytes=64)
         nc.vector.memset(w4_plane[:].bitcast(I32), 0)
@@ -67,7 +90,7 @@ def tile_list_jaw_scatter_correction_kernel(
         def load_w1(a, blocks):
             cols = slice(blocks[0] * PASS, (blocks[-1] + 1) * PASS)
             name = "w_raw%d%d" % (a, blocks[0])
-            raw = keep.tile([P, PACK, len(blocks) * PASS], F32, name=name, tag=name, align_bytes=64)
+            raw = place([P, PACK, len(blocks) * PASS], F32, name)
             rows = w1[a * PASS : (a + 1) * PASS, cols]
             nc.sync.dma_start(raw[:], rows.rearrange("(p j) c -> p j c", j=PACK))
             for i, b in enumerate(blocks):
@@ -81,20 +104,21 @@ def tile_list_jaw_scatter_correction_kernel(
             tab[a] = words
 
         load_tab(0)
+        nc.sync.dma_start(offsets[:], offs)
         nc.sync.dma_start(gain_rows[0:BLOCKS, :], gain.rearrange("(b r) -> b r", b=BLOCKS))
-        load_w1(0, (0, 1))
+        load_tab(1)
         for q in range(QUADRANTS):
             nc.sync.dma_start(
                 tab_plane[QUADRANT * q : QUADRANT * q + PLANE_ROWS * PASSES, :].bitcast(I32),
                 tab_scales[:, PLANE_ROWS * q : PLANE_ROWS * (q + 1), :].bitcast(I32),
             )
+        load_w1(0, (0, 1))
         load_w1(1, (0, 1))
-        load_tab(1)
         load_tab(2)
         load_w1(2, (0,))
         load_w1(2, (1,))
 
-        readings = []
+        readings = {}
         w4_codes = {}
 
         def load_w4(tiles):
@@ -110,14 +134,14 @@ def tile_list_jaw_scatter_correction_kernel(
                     first = b * width + i * FP4_BYTES * P
                     w4_codes[b, c] = codes[:, first : first + FP4_BYTES * P]
 
-        for c in range(VIEW_TILES):
+        for i, c in enumerate(LOAD_ORDER):
             rows = keep.tile([P, T], F32, name="readings%d" % c)
             nc.sync.dma_start(rows[:], gT[c * P : (c + 1) * P, :])
-            readings.append(rows)
-            if c == VIEW_TILES - 1:
-                load_w4(range(4, VIEW_TILES))
-                load_w4(range(0, 4))
-            if c == W4_AFTER + 1:
+            readings[c] = rows
+            if i == VIEW_TILES - 1:
+                load_w4(range(VIEW_TILES - 1, VIEW_TILES))
+                load_w4(range(0, VIEW_TILES - 1))
+            if i == W4_AFTER + 1:
                 nc.sync.dma_start(air_rows[0:VIEW_TILES, :], air.rearrange("(c p) -> c p", p=P))
                 for q in range(QUADRANTS):
                     nc.sync.dma_start(
@@ -134,53 +158,70 @@ def tile_list_jaw_scatter_correction_kernel(
         gain_bank = bank(BANKS - 1)
         for t in range(PACK):
             nc.tensor.transpose(gain_bank[:, t * P : (t + 1) * P], gain_rows[:, t:PASS:PACK], identity[:])
-        gain_cols = keep.tile([P, BLOCKS, PACK], F32, name="gain_cols")
+        gain_cols = keep.tile([P, BLOCKS, PACK], F32, name="gain_cols", tag="rounded", align_bytes=64)
         nc.scalar.copy(gain_cols[:], gain_bank[:].rearrange("p (t b) -> p b t", t=PACK)[:, 0:BLOCKS, :])
         gain_flat = gain_cols[:].rearrange("p b t -> p (b t)")
         gain_rsqrt = keep.tile([P, BLOCKS * PACK], F32, name="gain_rsqrt")
         nc.scalar.activation(gain_rsqrt[:], gain_flat, ACT.Abs_reciprocal_sqrt)
         gain_root = keep.tile([P, BLOCKS * PACK], F32, name="gain_root")
-        nc.gpsimd.tensor_tensor(gain_root[:], gain_flat, gain_rsqrt[:], MULT)
+        for col in range(BLOCKS * PACK):
+            one = slice(col, col + 1)
+            nc.scalar.activation(gain_root[:, one], gain_rsqrt[:, one], ACT.Copy, scale=gain_flat[:, one])
 
-        air_cols = keep.tile([P, VIEW_TILES], F32, name="air_cols")
 
         w_codes, w_plane, v_words = {}, {}, {}
 
-        def quantise_w1(a, b, shares):
-            rounded = ring.tile([P, PACK * PASS], BF16, name="w_rounded", bufs=3, align_bytes=64)
-            for copy, groups in shares:
-                copy(
-                    rounded[:].rearrange("p (t m j) -> p m j t", t=PACK, j=PACK)[:, groups],
-                    w_raw[a, b].rearrange("p j (m t) -> p m j t", t=PACK)[:, groups],
+        def quantise_w1(a, blocks, shares):
+            width = len(blocks) * PASS
+            name = "%d%d" % (a, blocks[0])
+            tag = "w_raw20" if name == "21" else "rounded"
+            rounded = place([P, PACK * width], BF16, "rounded" + name, tag)
+            for i, b in enumerate(blocks):
+                part = rounded[:, i * PACK * PASS : (i + 1) * PACK * PASS]
+                for copy, groups in shares[i]:
+                    copy(
+                        part.rearrange("p (t m j) -> p m j t", t=PACK, j=PACK)[:, groups],
+                        w_raw[a, b].rearrange("p j (m t) -> p m j t", t=PACK)[:, groups],
+                    )
+            codes = place([P, width], U32, "w_codes" + name)
+            plane = place([P, width], U8, "w_plane" + name)
+            for i, b in enumerate(blocks):
+                w_codes[a, b] = codes[:, i * PASS : (i + 1) * PASS]
+                w_plane[a, b] = plane[:, i * PASS : (i + 1) * PASS]
+
+            def quantise(first, last):
+                nc.vector.quantize_mx(
+                    out=codes[:, first * PASS : last * PASS].bitcast(FP8X4),
+                    scales=plane[:, first * PASS : last * PASS],
+                    in_=rounded[:, first * PACK * PASS : last * PACK * PASS],
                 )
-            tag = "tab%d" % (1 + b) if a == 1 else "w_codes%d%d" % (a, b)
-            codes = keep.tile([P, PASS], U32, name="w_codes%d%d" % (a, b), tag=tag, align_bytes=64)
-            tag = "tab_plane" if (a, b) == (0, 0) else "w_plane%d%d" % (a, b)
-            plane = keep.tile([P, PASS], U8, name="w_plane%d%d" % (a, b), tag=tag, align_bytes=64)
-            nc.vector.quantize_mx(out=codes[:].bitcast(FP8X4), scales=plane[:], in_=rounded[:])
-            w_codes[a, b], w_plane[a, b] = codes, plane
 
-        def gather_words(a):
-            words = keep.tile([P, S], U32, name="v_words%d" % a, align_bytes=64)
-            nc.vector.tensor_copy(words[:], tab[a][:].indirect(offsets[:]))
-            v_words[a] = words
+            return quantise
 
-        gather_words(0)
+        def gather_words(passes):
+            words = place([P, len(passes), S], U32, "v_words%d" % passes[0])
+            for i, a in enumerate(passes):
+                nc.vector.tensor_copy(words[:, i, :], tab[a][:].indirect(offsets[:]))
+                for half in range(HALVES):
+                    v_words[a, half] = words[:, i, half * HALF : (half + 1) * HALF]
+
+        gather_words((0,))
+        gather_words((1,))
         v_plane = keep.tile([P, S], U8, name="v_plane", align_bytes=64)
         nc.vector.tensor_copy(v_plane[:], tab_plane[:].indirect(offsets[:]))
 
         h_banks = {}
 
-        def first_product(a, b, half):
+        def first_product(a, b, half, slots):
             cols = slice(half * HALF, (half + 1) * HALF)
-            for t in range(PACK):
+            for t in slots:
                 if a == 0:
                     h_banks[b, half, t] = bank(PACK * b + t)
                 nc.tensor.matmul_mx(
                     out=h_banks[b, half, t][:],
                     lhsT=w_codes[a, b][:, t * P : (t + 1) * P].bitcast(FP8X4),
                     lhsT_scale=w_plane[a, b][:, t * P : (t + 1) * P],
-                    rhs=v_words[a][:, cols].bitcast(FP8X4),
+                    rhs=v_words[a, half].bitcast(FP8X4),
                     rhs_scale=v_plane[PLANE_ROWS * a : P, cols],
                     start=(a == 0),
                     stop=(a == PASSES - 1),
@@ -188,14 +229,13 @@ def tile_list_jaw_scatter_correction_kernel(
 
         z_rows, z_woven, z_codes, z_plane = {}, {}, {}, {}
 
-        def energies(b, half):
-            if (b, half) == (BLOCKS - 1, HALVES - 1):
-                rows = keep.tile([P, PACK, HALF], BF16, name="z_rows_last", tag="first_root")
-            elif (b, half) == (0, 0):
-                rows = keep.tile([P, PACK, HALF], BF16, name="z_rows_first", tag="w_raw21", align_bytes=64)
+        def energies(b, half, slots):
+            name = "z_rows%d%d" % (b, half)
+            if (b, half) in z_rows:
+                rows = z_rows[b, half]
             else:
-                rows = ring.tile([P, PACK, HALF], BF16, name="z_rows")
-            for t in range(PACK):
+                rows = place([P, PACK, HALF], BF16, name, "w_raw10")
+            for t in slots:
                 col = PACK * b + t
                 nc.scalar.activation(
                     rows[:, t, :], h_banks[b, half, t][:], ACT.Square, scale=gain_root[:, col : col + 1]
@@ -204,7 +244,9 @@ def tile_list_jaw_scatter_correction_kernel(
 
         def weave_z(b, half):
             if b == 0:
-                z_woven[half] = ring.tile([P, BLOCKS * PACK * HALF], BF16, name="z_woven", align_bytes=64)
+                z_woven[half] = keep.tile(
+                    [P, BLOCKS * PACK * HALF], BF16, name="z_woven%d" % half, tag=("w_raw00", "tab0")[half], align_bytes=64
+                )
             nc.scalar.copy(
                 z_woven[half][:, b * PACK * HALF : (b + 1) * PACK * HALF].rearrange(
                     "p (c i t) -> p c t i", i=RUN, t=PACK
@@ -221,34 +263,23 @@ def tile_list_jaw_scatter_correction_kernel(
 
         picked = {}
 
-        def gather_readings(c):
-            tag = ("tab0", "w_raw00", "w_raw10", "w_raw20", "w_raw21", "picked5")[c]
-            values = keep.tile([P, S], F32, name="picked%d" % c, tag=tag, align_bytes=64)
-            nc.vector.tensor_copy(values[:], readings[c][:].indirect(offsets[:]))
-            picked[c] = values
+        def gather_readings():
+            early = place([P, EARLY_TILES, S], F32, "picked")
+            late = place([P, VIEW_TILES - EARLY_TILES, S], F32, "picked_late")
+            for i, c in enumerate(LOAD_ORDER):
+                picked[c] = early[:, i, :] if i < EARLY_TILES else late[:, i - EARLY_TILES, :]
+                nc.vector.tensor_copy(picked[c], readings[c][:].indirect(offsets[:]))
 
         inverse = {}
 
-        def second_product(c, half, number):
-            y_bank = bank(number)
-            for b in range(BLOCKS):
-                first = b * N + c * P
-                nc.tensor.matmul_mx(
-                    out=y_bank[:],
-                    lhsT=w4_codes[b, c].bitcast(FP4X4),
-                    lhsT_scale=w4_plane[:, first : first + P],
-                    rhs=z_codes[half][:, b * HALF : (b + 1) * HALF].bitcast(FP8X4),
-                    rhs_scale=z_plane[half][:, b * HALF : (b + 1) * HALF],
-                    start=(b == 0),
-                    stop=(b == BLOCKS - 1),
-                )
-            first_of_all = (c, half) == (SPLIT_TILES[0], 0)
-            if half == 0 and c in SPLIT_TILES[:2]:
-                root = keep.tile([P, HALF], F32, name="first_root", tag="first_root")
+        def second_product(c, half, numbers):
+            width = HALF // len(numbers)
+            if half == 0 and c in SPLIT_TILES[:AHEAD]:
+                root = keep.tile([P, HALF], F32, name="first_root", tag="tab0", align_bytes=64)
             else:
-                root = ring.tile([P, HALF], F32, name="root")
-            nc.scalar.activation(root[:], y_bank[:], ACT.Abs_reciprocal_sqrt, bias=air_cols[:, c : c + 1])
-            if first_of_all:
+                name = "root%d%d" % (c, half)
+                root = shared.tile([P, HALF], F32, name=name, offset=PLACE["z_rows01"], align_bytes=64)
+            if (c, half) == (SPLIT_TILES[0], 0):
                 whole = keep.tile([P, HALF], F32, name="first_inverse", tag="first_inverse", align_bytes=64)
                 inverse[c, half] = whole[:]
             elif c in SPLIT_TILES:
@@ -258,7 +289,29 @@ def tile_list_jaw_scatter_correction_kernel(
                 whole = ring.tile([P, S], F32, name="inverse")
                 inverse[c] = whole[:]
                 inverse[c, 0], inverse[c, 1] = whole[:, 0:HALF], whole[:, HALF:S]
-            nc.scalar.activation(inverse[c, half], root[:], ACT.Square)
+            for i, number in enumerate(numbers):
+                y_bank = bank(number)
+                for b in range(BLOCKS):
+                    first = b * N + c * P
+                    entries = slice(b * HALF + i * width, b * HALF + (i + 1) * width)
+                    nc.tensor.matmul_mx(
+                        out=y_bank[:, 0:width],
+                        lhsT=w4_codes[b, c].bitcast(FP4X4),
+                        lhsT_scale=w4_plane[:, first : first + P],
+                        rhs=z_codes[half][:, entries].bitcast(FP8X4),
+                        rhs_scale=z_plane[half][:, entries],
+                        start=(b == 0),
+                        stop=(b == BLOCKS - 1),
+                    )
+                nc.scalar.activation(
+                    root[:, i * width : (i + 1) * width],
+                    y_bank[:, 0:width],
+                    ACT.Abs_reciprocal_sqrt,
+                    bias=air_cols[:, c : c + 1],
+                )
+            for i in range(len(numbers)):
+                part = slice(i * width, (i + 1) * width)
+                nc.scalar.activation(inverse[c, half][:, part], root[:, part], ACT.Square)
 
         def scatter(c, halves):
             start, stop = halves.start * HALF, halves.stop * HALF
@@ -273,52 +326,60 @@ def tile_list_jaw_scatter_correction_kernel(
             nc.sync.dma_start(out[c * P : (c + 1) * P, :], readings[c][:])
 
         on_scalar = [(nc.scalar.copy, slice(0, P))]
-        shared = [(nc.vector.tensor_copy, slice(0, VECTOR_GROUPS)), (nc.scalar.copy, slice(VECTOR_GROUPS, P))]
+        on_vector = [(nc.vector.tensor_copy, slice(0, P))]
+
+        def on_both(groups):
+            return [(nc.vector.tensor_copy, slice(0, groups)), (nc.scalar.copy, slice(groups, P))]
+
+        quantise_w1(0, (0, 1), (on_scalar, on_vector))(0, 2)
+        quantise = quantise_w1(1, (0, 1), (on_scalar, on_vector))
+        quantise(1, 2)
+        gather_words((2,))
+        quantise(0, 1)
         for a in range(PASSES):
-            if a == 1:
-                gather_words(1)
-                gather_words(2)
-            quantise_w1(a, 0, on_scalar)
-            first_product(a, 0, 0)
-            quantise_w1(a, 1, shared if a == PASSES - 1 else on_scalar)
-            first_product(a, 1, 0)
-        energies(0, 0)
+            for b in range(BLOCKS):
+                if a == PASSES - 1:
+                    quantise_w1(a, (b,), (on_both(VECTOR_GROUPS[b]),))(0, 1)
+                first_product(a, b, 0, range(PACK))
+        energies(0, 0, range(PACK))
+        energies(1, 0, range(PACK))
         weave_z(0, 0)
-        energies(1, 0)
         weave_z(1, 0)
 
+        air_cols = keep.tile([P, VIEW_TILES], F32, name="air_cols")
         air_bank = bank(BANKS - 1)
         nc.tensor.transpose(air_bank[:, 0:P], air_rows[:], identity[:])
         nc.scalar.copy(air_cols[:], air_bank[:, 0:VIEW_TILES])
         quantise_z(0)
 
-        for a in range(PASSES):
-            first_product(a, 0, 1)
-        for c in range(VIEW_TILES):
-            gather_readings(c)
-        energies(0, 1)
+        for b in range(BLOCKS):
+            for t in range(PACK):
+                for a in range(PASSES):
+                    first_product(a, b, 1, (t,))
+        gather_readings()
+        energies(0, 1, range(PACK))
+        energies(1, 1, range(PACK))
 
-        for i, c in enumerate(SPLIT_TILES[:-1]):
-            second_product(c, 0, (0, BANKS - 1)[i])
-            scatter(c, range(0, 1))
-        for a in range(PASSES):
-            first_product(a, 1, 1)
+        second_product(SPLIT_TILES[0], 0, (0, 1))
+        scatter(SPLIT_TILES[0], range(0, 1))
+        second_product(SPLIT_TILES[1], 0, (2,))
+        scatter(SPLIT_TILES[1], range(0, 1))
         weave_z(0, 1)
-        energies(1, 1)
         weave_z(1, 1)
         quantise_z(1)
-        second_product(SPLIT_TILES[-1], 0, BANKS - 1)
-        scatter(SPLIT_TILES[-1], range(0, 1))
+        second_product(SPLIT_TILES[2], 0, (3,))
+        scatter(SPLIT_TILES[2], range(0, 1))
 
-        next_bank = 1
-        for c in SPLIT_TILES:
-            second_product(c, 1, next_bank % BANKS)
-            next_bank = next_bank + 1
+        next_bank = PACK
+        for i, c in enumerate(SPLIT_TILES):
+            count = 2 if i == 0 else 1
+            second_product(c, 1, range(next_bank, next_bank + count))
+            next_bank = next_bank + count
             scatter(c, range(1, HALVES))
             store(c)
         for c in range(VIEW_TILES - len(SPLIT_TILES)):
             for half in range(HALVES):
-                second_product(c, half, next_bank % BANKS)
+                second_product(c, half, (next_bank % BANKS,))
                 next_bank = next_bank + 1
             scatter(c, range(0, HALVES))
             store(c)

@@ -31,7 +31,7 @@ QUADRANT = P // QUADRANTS
 PLANE_ROWS = 4
 FP4_BYTES = 2
 BANKS = 8
-VECTOR_GROUPS = (56, 64)
+VECTOR_GROUPS = (84, 72)
 RUN = 4
 INVERSE_TILES = 4
 W4_AFTER = 2
@@ -43,15 +43,16 @@ PLACE = {
     "picked_late": 0,
     "z_rows10": 6 * KIB,
     "z_rows01": 8 * KIB,
-    "w_raw21": 12 * KIB,
+    "w_raw20": 12 * KIB,
     "z_rows00": 12 * KIB,
-    "picked": 16 * KIB,
-    "tab_plane": 32 * KIB,
-    "w_plane00": 32 * KIB,
-    "w_raw10": 37 * KIB,
-    "v_words2": 37 * KIB,
-    "rounded20": 41 * KIB,
-    "z_rows11": 41 * KIB,
+    "picked": 20 * KIB,
+    "w_raw10": 34 * KIB,
+    "rounded20": 34 * KIB,
+    "rounded21": 38 * KIB,
+    "z_rows11": 38 * KIB,
+    "v_words2": 42 * KIB,
+    "tab_plane": 50 * KIB,
+    "w_plane00": 50 * KIB,
 }
 EARLY_TILES = 4
 
@@ -87,14 +88,25 @@ def tile_list_jaw_scatter_correction_kernel(
 
         w_raw, tab = {}, {}
 
-        def load_w1(a, blocks):
-            cols = slice(blocks[0] * PASS, (blocks[-1] + 1) * PASS)
-            name = "w_raw%d%d" % (a, blocks[0])
-            raw = place([P, PACK, len(blocks) * PASS], F32, name)
-            rows = w1[a * PASS : (a + 1) * PASS, cols]
-            nc.sync.dma_start(raw[:], rows.rearrange("(p j) c -> p j c", j=PACK))
-            for i, b in enumerate(blocks):
-                w_raw[a, b] = raw[:, :, i * PASS : (i + 1) * PASS]
+        def load_w1(a):
+            raw = place([P, 2, 2, H], F32, "w_raw%d0" % a)
+            rows = w1[a * PASS : (a + 1) * PASS, :]
+            nc.sync.dma_start(
+                raw[:].rearrange("p u e c -> p (u e c)"), rows.rearrange("(p j) c -> p (j c)", j=PACK)
+            )
+            for b in range(BLOCKS):
+                w_raw[a, b] = raw[:, :, :, b * PASS : (b + 1) * PASS]
+
+        def load_last_w1(a):
+            raw = place([P, 11, PASS], F32, "w_raw%d0" % a)
+            runs = w1[a * PASS : (a + 1) * PASS, :].rearrange("(p u e) (b c) -> p u (e b) c", u=2, e=2, b=BLOCKS)
+            first = raw[:, 0:6, :].rearrange("p (u r) c -> p u r c", u=2)
+            nc.sync.dma_start(
+                first.rearrange("p u r c -> p u (r c)"), runs[:, :, 0:3, :].rearrange("p u r c -> p u (r c)")
+            )
+            nc.sync.dma_start(raw[:, 6:10:3, :], runs[:, :, 3, :])
+            w_raw[a, 0] = first[:, :, 0:3:2, :]
+            w_raw[a, 1] = raw[:, 1:11, :].rearrange("p (e r) c -> p r e c", e=2)[:, 0:4:3, :, :]
 
         def load_tab(a):
             words = keep.tile([P, T], U32, name="tab%d" % a, tag="tab%d" % a, align_bytes=64)
@@ -112,11 +124,10 @@ def tile_list_jaw_scatter_correction_kernel(
                 tab_plane[QUADRANT * q : QUADRANT * q + PLANE_ROWS * PASSES, :].bitcast(I32),
                 tab_scales[:, PLANE_ROWS * q : PLANE_ROWS * (q + 1), :].bitcast(I32),
             )
-        load_w1(0, (0, 1))
-        load_w1(1, (0, 1))
+        load_w1(0)
+        load_w1(1)
         load_tab(2)
-        load_w1(2, (0,))
-        load_w1(2, (1,))
+        load_last_w1(2)
 
         readings = {}
         w4_codes = {}
@@ -174,14 +185,13 @@ def tile_list_jaw_scatter_correction_kernel(
         def quantise_w1(a, blocks, shares):
             width = len(blocks) * PASS
             name = "%d%d" % (a, blocks[0])
-            tag = "w_raw20" if name == "21" else "rounded"
-            rounded = place([P, PACK * width], BF16, "rounded" + name, tag)
+            rounded = place([P, PACK * width], BF16, "rounded" + name, "rounded")
             for i, b in enumerate(blocks):
                 part = rounded[:, i * PACK * PASS : (i + 1) * PACK * PASS]
                 for copy, groups in shares[i]:
                     copy(
-                        part.rearrange("p (t m j) -> p m j t", t=PACK, j=PACK)[:, groups],
-                        w_raw[a, b].rearrange("p j (m t) -> p m j t", t=PACK)[:, groups],
+                        part.rearrange("p (t m u e) -> p m u e t", t=PACK, u=2, e=2)[:, groups],
+                        w_raw[a, b].rearrange("p u e (m t) -> p m u e t", t=PACK)[:, groups],
                     )
             codes = place([P, width], U32, "w_codes" + name)
             plane = place([P, width], U8, "w_plane" + name)

@@ -119,7 +119,7 @@ def tile_list_jaw_scatter_correction_kernel(
         nc.sync.dma_start(offsets[:], offs)
         nc.sync.dma_start(gain_rows[0:BLOCKS, :], gain.rearrange("(b r) -> b r", b=BLOCKS))
         load_tab(1)
-        for q in range(QUADRANTS):
+        for q in reversed(range(QUADRANTS)):
             nc.sync.dma_start(
                 tab_plane[QUADRANT * q : QUADRANT * q + PLANE_ROWS * PASSES, :].bitcast(I32),
                 tab_scales[:, PLANE_ROWS * q : PLANE_ROWS * (q + 1), :].bitcast(I32),

@@ -31,7 +31,7 @@ QUADRANT = P // QUADRANTS
 PLANE_ROWS = 4
 FP4_BYTES = 2
 BANKS = 8
-VECTOR_GROUPS = (84, 72)
+VECTOR_GROUPS = (84, 84)
 RUN = 4
 INVERSE_TILES = 4
 W4_AFTER = 2
@@ -98,15 +98,12 @@ def tile_list_jaw_scatter_correction_kernel(
                 w_raw[a, b] = raw[:, :, :, b * PASS : (b + 1) * PASS]
 
         def load_last_w1(a):
-            raw = place([P, 11, PASS], F32, "w_raw%d0" % a)
-            runs = w1[a * PASS : (a + 1) * PASS, :].rearrange("(p u e) (b c) -> p u (e b) c", u=2, e=2, b=BLOCKS)
-            first = raw[:, 0:6, :].rearrange("p (u r) c -> p u r c", u=2)
-            nc.sync.dma_start(
-                first.rearrange("p u r c -> p u (r c)"), runs[:, :, 0:3, :].rearrange("p u r c -> p u (r c)")
-            )
-            nc.sync.dma_start(raw[:, 6:10:3, :], runs[:, :, 3, :])
-            w_raw[a, 0] = first[:, :, 0:3:2, :]
-            w_raw[a, 1] = raw[:, 1:11, :].rearrange("p (e r) c -> p r e c", e=2)[:, 0:4:3, :, :]
+            raw = place([P, 2, 2, H], F32, "w_raw%d0" % a)
+            rows = w1[a * PASS : (a + 1) * PASS, :].rearrange("(p j) c -> p (j c)", j=PACK)
+            for part in (slice(0, PACK * H - PASS), slice(PACK * H - PASS, PACK * H)):
+                nc.sync.dma_start(raw[:].rearrange("p u e c -> p (u e c)")[:, part], rows[:, part])
+            for b in range(BLOCKS):
+                w_raw[a, b] = raw[:, :, :, b * PASS : (b + 1) * PASS]
 
         def load_tab(a):
             words = keep.tile([P, T], U32, name="tab%d" % a, tag="tab%d" % a, align_bytes=64)
@@ -201,9 +198,9 @@ def tile_list_jaw_scatter_correction_kernel(
 
             def quantise(first, last):
                 nc.vector.quantize_mx(
-                    out=codes[:, first * PASS : last * PASS].bitcast(FP8X4),
-                    scales=plane[:, first * PASS : last * PASS],
-                    in_=rounded[:, first * PACK * PASS : last * PACK * PASS],
+                    out=codes[:, first * P : last * P].bitcast(FP8X4),
+                    scales=plane[:, first * P : last * P],
+                    in_=rounded[:, first * PASS : last * PASS],
                 )
 
             return quantise
@@ -264,11 +261,17 @@ def tile_list_jaw_scatter_correction_kernel(
                 z_rows[b, half][:].rearrange("p t (c i) -> p c t i", i=RUN),
             )
 
-        def quantise_z(half):
+        def quantise_z(half, calls):
             codes = keep.tile([P, BLOCKS * HALF], U32, name="z_codes%d" % half, align_bytes=64)
             tag = "air_rows" if half == 0 else "first_inverse"
             plane = keep.tile([P, BLOCKS * HALF], U8, name="z_plane%d" % half, tag=tag, align_bytes=64)
-            nc.vector.quantize_mx(out=codes[:].bitcast(FP8X4), scales=plane[:], in_=z_woven[half][:])
+            width = BLOCKS * HALF // calls
+            for first in range(0, BLOCKS * HALF, width):
+                nc.vector.quantize_mx(
+                    out=codes[:, first : first + width].bitcast(FP8X4),
+                    scales=plane[:, first : first + width],
+                    in_=z_woven[half][:, PACK * first : PACK * (first + width)],
+                )
             z_codes[half], z_plane[half] = codes, plane
 
         picked = {}
@@ -341,15 +344,18 @@ def tile_list_jaw_scatter_correction_kernel(
         def on_both(groups):
             return [(nc.vector.tensor_copy, slice(0, groups)), (nc.scalar.copy, slice(groups, P))]
 
-        quantise_w1(0, (0, 1), (on_scalar, on_vector))(0, 2)
+        quantise_w1(0, (0, 1), (on_scalar, on_vector))(0, 2 * PACK)
         quantise = quantise_w1(1, (0, 1), (on_scalar, on_vector))
-        quantise(1, 2)
+        quantise(PACK, 2 * PACK)
         gather_words((2,))
-        quantise(0, 1)
+        quantise(0, PACK)
         for a in range(PASSES):
             for b in range(BLOCKS):
                 if a == PASSES - 1:
-                    quantise_w1(a, (b,), (on_both(VECTOR_GROUPS[b]),))(0, 1)
+                    quantise = quantise_w1(a, (b,), (on_both(VECTOR_GROUPS[b]),))
+                    step = PACK // 2 if b == 0 else PACK
+                    for first in range(0, PACK, step):
+                        quantise(first, first + step)
                 first_product(a, b, 0, range(PACK))
         energies(0, 0, range(PACK))
         energies(1, 0, range(PACK))
@@ -360,7 +366,7 @@ def tile_list_jaw_scatter_correction_kernel(
         air_bank = bank(BANKS - 1)
         nc.tensor.transpose(air_bank[:, 0:P], air_rows[:], identity[:])
         nc.scalar.copy(air_cols[:], air_bank[:, 0:VIEW_TILES])
-        quantise_z(0)
+        quantise_z(0, BLOCKS)
 
         for b in range(BLOCKS):
             for t in range(PACK):
@@ -376,7 +382,7 @@ def tile_list_jaw_scatter_correction_kernel(
         scatter(SPLIT_TILES[1], range(0, 1))
         weave_z(0, 1)
         weave_z(1, 1)
-        quantise_z(1)
+        quantise_z(1, 1)
         second_product(SPLIT_TILES[2], 0, (3,))
         scatter(SPLIT_TILES[2], range(0, 1))
 

@@ -31,7 +31,7 @@ QUADRANT = P // QUADRANTS
 PLANE_ROWS = 4
 FP4_BYTES = 2
 BANKS = 8
-VECTOR_GROUPS = (84, 84)
+VECTOR_GROUPS = (96, 56)
 RUN = 4
 INVERSE_TILES = 4
 W4_AFTER = 2
@@ -142,24 +142,25 @@ def tile_list_jaw_scatter_correction_kernel(
                     first = b * width + i * FP4_BYTES * P
                     w4_codes[b, c] = codes[:, first : first + FP4_BYTES * P]
 
+        def load_w4_scales(quadrants):
+            for q in quadrants:
+                nc.sync.dma_start(
+                    w4_plane[QUADRANT * q : QUADRANT * q + PLANE_ROWS, :]
+                    .bitcast(I32)
+                    .rearrange("r (b w) -> r b w", b=BLOCKS),
+                    w4_scales[:, PLANE_ROWS * q : PLANE_ROWS * (q + 1), :].bitcast(I32).rearrange("b r w -> r b w"),
+                )
+
         for i, c in enumerate(LOAD_ORDER):
             rows = keep.tile([P, T], F32, name="readings%d" % c)
             nc.sync.dma_start(rows[:], gT[c * P : (c + 1) * P, :])
             readings[c] = rows
-            if i == VIEW_TILES - 1:
-                load_w4(range(VIEW_TILES - 1, VIEW_TILES))
-                load_w4(range(0, VIEW_TILES - 1))
             if i == W4_AFTER + 1:
                 nc.sync.dma_start(air_rows[0:VIEW_TILES, :], air.rearrange("(c p) -> c p", p=P))
-                for q in range(QUADRANTS):
-                    nc.sync.dma_start(
-                        w4_plane[QUADRANT * q : QUADRANT * q + PLANE_ROWS, :]
-                        .bitcast(I32)
-                        .rearrange("r (b w) -> r b w", b=BLOCKS),
-                        w4_scales[:, PLANE_ROWS * q : PLANE_ROWS * (q + 1), :]
-                        .bitcast(I32)
-                        .rearrange("b r w -> r b w"),
-                    )
+                load_w4_scales(range(0, QUADRANTS // 2))
+        load_w4_scales(range(QUADRANTS // 2, QUADRANTS))
+        load_w4(range(VIEW_TILES - 1, VIEW_TILES))
+        load_w4(range(0, VIEW_TILES - 1))
 
         identity = keep.tile([P, P], F32, name="identity")
         make_identity(nc, identity[:])

@@ -51,6 +51,7 @@ PLACE = {
     "rounded21": 38 * KIB,
     "z_rows11": 38 * KIB,
     "v_words2": 42 * KIB,
+    "gain_rsqrt": 46 * KIB,
     "tab_plane": 50 * KIB,
     "w_plane00": 50 * KIB,
 }
@@ -114,13 +115,13 @@ def tile_list_jaw_scatter_correction_kernel(
 
         load_tab(0)
         nc.sync.dma_start(offsets[:], offs)
-        nc.sync.dma_start(gain_rows[0:BLOCKS, :], gain.rearrange("(b r) -> b r", b=BLOCKS))
         load_tab(1)
         for q in reversed(range(QUADRANTS)):
             nc.sync.dma_start(
                 tab_plane[QUADRANT * q : QUADRANT * q + PLANE_ROWS * PASSES, :].bitcast(I32),
                 tab_scales[:, PLANE_ROWS * q : PLANE_ROWS * (q + 1), :].bitcast(I32),
             )
+        nc.sync.dma_start(gain_rows[0:BLOCKS, :], gain.rearrange("(b r) -> b r", b=BLOCKS))
         load_w1(0)
         load_w1(1)
         load_tab(2)
@@ -167,10 +168,10 @@ def tile_list_jaw_scatter_correction_kernel(
         gain_bank = bank(BANKS - 1)
         for t in range(PACK):
             nc.tensor.transpose(gain_bank[:, t * P : (t + 1) * P], gain_rows[:, t:PASS:PACK], identity[:])
-        gain_cols = keep.tile([P, BLOCKS, PACK], F32, name="gain_cols", tag="rounded", align_bytes=64)
+        gain_cols = keep.tile([P, BLOCKS, PACK], F32, name="gain_cols")
         nc.scalar.copy(gain_cols[:], gain_bank[:].rearrange("p (t b) -> p b t", t=PACK)[:, 0:BLOCKS, :])
         gain_flat = gain_cols[:].rearrange("p b t -> p (b t)")
-        gain_rsqrt = keep.tile([P, BLOCKS * PACK], F32, name="gain_rsqrt")
+        gain_rsqrt = place([P, BLOCKS * PACK], F32, "gain_rsqrt")
         nc.scalar.activation(gain_rsqrt[:], gain_flat, ACT.Abs_reciprocal_sqrt)
         gain_root = keep.tile([P, BLOCKS * PACK], F32, name="gain_root")
         for col in range(BLOCKS * PACK):

@@ -51,7 +51,7 @@ PLACE = {
     "rounded21": 38 * KIB,
     "z_rows11": 38 * KIB,
     "v_words2": 42 * KIB,
-    "gain_rsqrt": 46 * KIB,
+    "gain_root": 46 * KIB,
     "tab_plane": 50 * KIB,
     "w_plane00": 50 * KIB,
 }
@@ -121,7 +121,8 @@ def tile_list_jaw_scatter_correction_kernel(
                 tab_plane[QUADRANT * q : QUADRANT * q + PLANE_ROWS * PASSES, :].bitcast(I32),
                 tab_scales[:, PLANE_ROWS * q : PLANE_ROWS * (q + 1), :].bitcast(I32),
             )
-        nc.sync.dma_start(gain_rows[0:BLOCKS, :], gain.rearrange("(b r) -> b r", b=BLOCKS))
+            if q == QUADRANTS - 1:
+                nc.sync.dma_start(gain_rows[0:BLOCKS, :], gain.rearrange("(b r) -> b r", b=BLOCKS))
         load_w1(0)
         load_w1(1)
         load_tab(2)
@@ -168,12 +169,15 @@ def tile_list_jaw_scatter_correction_kernel(
         gain_bank = bank(BANKS - 1)
         for t in range(PACK):
             nc.tensor.transpose(gain_bank[:, t * P : (t + 1) * P], gain_rows[:, t:PASS:PACK], identity[:])
+        gain_turned = gain_bank[:].rearrange("p (t b) -> p b t", t=PACK)[:, 0:BLOCKS, :]
+        gain_rsqrt = keep.tile([P, BLOCKS * PACK], F32, name="gain_rsqrt")
+        nc.scalar.activation(
+            gain_rsqrt[:].rearrange("p (b t) -> p b t", t=PACK), gain_turned, ACT.Abs_reciprocal_sqrt
+        )
         gain_cols = keep.tile([P, BLOCKS, PACK], F32, name="gain_cols")
-        nc.scalar.copy(gain_cols[:], gain_bank[:].rearrange("p (t b) -> p b t", t=PACK)[:, 0:BLOCKS, :])
+        nc.scalar.copy(gain_cols[:], gain_turned)
         gain_flat = gain_cols[:].rearrange("p b t -> p (b t)")
-        gain_rsqrt = place([P, BLOCKS * PACK], F32, "gain_rsqrt")
-        nc.scalar.activation(gain_rsqrt[:], gain_flat, ACT.Abs_reciprocal_sqrt)
-        gain_root = keep.tile([P, BLOCKS * PACK], F32, name="gain_root")
+        gain_root = place([P, BLOCKS * PACK], F32, "gain_root")
         for col in range(BLOCKS * PACK):
             one = slice(col, col + 1)
             nc.scalar.activation(gain_root[:, one], gain_rsqrt[:, one], ACT.Copy, scale=gain_flat[:, one])

@@ -121,9 +121,8 @@ def tile_list_jaw_scatter_correction_kernel(
                 tab_plane[QUADRANT * q : QUADRANT * q + PLANE_ROWS * PASSES, :].bitcast(I32),
                 tab_scales[:, PLANE_ROWS * q : PLANE_ROWS * (q + 1), :].bitcast(I32),
             )
-            if q == QUADRANTS - 1:
-                nc.sync.dma_start(gain_rows[0:BLOCKS, :], gain.rearrange("(b r) -> b r", b=BLOCKS))
         load_w1(0)
+        nc.sync.dma_start(gain_rows[0:BLOCKS, :], gain.rearrange("(b r) -> b r", b=BLOCKS))
         load_w1(1)
         load_tab(2)
         load_last_w1(2)
@@ -170,13 +169,10 @@ def tile_list_jaw_scatter_correction_kernel(
         for t in range(PACK):
             nc.tensor.transpose(gain_bank[:, t * P : (t + 1) * P], gain_rows[:, t:PASS:PACK], identity[:])
         gain_turned = gain_bank[:].rearrange("p (t b) -> p b t", t=PACK)[:, 0:BLOCKS, :]
-        gain_rsqrt = keep.tile([P, BLOCKS * PACK], F32, name="gain_rsqrt")
-        nc.scalar.activation(
-            gain_rsqrt[:].rearrange("p (b t) -> p b t", t=PACK), gain_turned, ACT.Abs_reciprocal_sqrt
-        )
-        gain_cols = keep.tile([P, BLOCKS, PACK], F32, name="gain_cols")
-        nc.scalar.copy(gain_cols[:], gain_turned)
-        gain_flat = gain_cols[:].rearrange("p b t -> p (b t)")
+        gain_work = keep.tile([P, 2, BLOCKS * PACK], F32, name="gain_work", tag="w_raw00", align_bytes=64)
+        gain_rsqrt, gain_flat = gain_work[:, 0, :], gain_work[:, 1, :]
+        nc.scalar.activation(gain_rsqrt.rearrange("p (b t) -> p b t", t=PACK), gain_turned, ACT.Abs_reciprocal_sqrt)
+        nc.scalar.copy(gain_flat.rearrange("p (b t) -> p b t", t=PACK), gain_turned)
         gain_root = place([P, BLOCKS * PACK], F32, "gain_root")
         for col in range(BLOCKS * PACK):
             one = slice(col, col + 1)

@@ -78,14 +78,14 @@ def tile_list_jaw_scatter_correction_kernel(
 
         offsets = keep.tile([P, S // LIST_GROUP], U16, name="offsets")
 
-        gain_rows = keep.tile([P, PASS], F32, name="gain_rows")
-        nc.vector.memset(gain_rows[:], 0.0)
         tab_plane = place([P, T], U8, "tab_plane")
         nc.gpsimd.memset(tab_plane[:].bitcast(I32), 0)
-        w4_plane = keep.tile([P, BLOCKS * N], U8, name="w4_plane", align_bytes=64)
-        nc.vector.memset(w4_plane[:].bitcast(I32), 0)
+        gain_rows = keep.tile([P, PASS], F32, name="gain_rows")
+        nc.gpsimd.memset(gain_rows[:], 0.0)
         air_rows = keep.tile([P, P], F32, name="air_rows", tag="air_rows", align_bytes=64)
         nc.gpsimd.memset(air_rows[:], 0.0)
+        w4_plane = keep.tile([P, BLOCKS * N], U8, name="w4_plane", align_bytes=64)
+        nc.gpsimd.memset(w4_plane[:].bitcast(I32), 0)
 
         w_raw, tab = {}, {}
 

from contextlib import ExitStack

import concourse.mybir as mybir
from concourse.masks import make_identity

K, H, N, T, S = 1536, 1024, 768, 2048, 1024
FLOPS = 2 * K * H * S + 2 * H * N * S

F32 = mybir.dt.float32
BF16 = mybir.dt.bfloat16
I32 = mybir.dt.int32
U32 = mybir.dt.uint32
U16 = mybir.dt.uint16
U8 = mybir.dt.uint8
FP8X4 = mybir.dt.float8_e4m3fn_x4
FP4X4 = mybir.dt.float4_e2m1fn_x4
ACT = mybir.ActivationFunctionType
MULT = mybir.AluOpType.mult

P = 128
PACK = 4
PASS = P * PACK
PASSES = K // PASS
BLOCKS = H // PASS
VIEW_TILES = N // P
HALF = 512
HALVES = S // HALF
LIST_GROUP = 16
QUADRANTS = 4
QUADRANT = P // QUADRANTS
PLANE_ROWS = 4
FP4_BYTES = 2
BANKS = 8
VECTOR_GROUPS = (96, 56)
RUN = 4
INVERSE_TILES = 4
W4_AFTER = 2
SPLIT_TILES = (5, 4, 3)
LOAD_ORDER = (0, 1, 2, 3, 5, 4)
AHEAD = 2
KIB = 1024
PLACE = {
    "picked_late": 0,
    "z_rows10": 6 * KIB,
    "z_rows01": 8 * KIB,
    "w_raw20": 12 * KIB,
    "z_rows00": 12 * KIB,
    "picked": 20 * KIB,
    "w_raw10": 34 * KIB,
    "rounded20": 34 * KIB,
    "rounded21": 38 * KIB,
    "z_rows11": 38 * KIB,
    "v_words2": 42 * KIB,
    "gain_root": 46 * KIB,
    "tab_plane": 50 * KIB,
    "w_plane00": 50 * KIB,
}
EARLY_TILES = 4


def tile_list_jaw_scatter_correction_kernel(
    tc, tab_words, tab_scales, w1, w4_words, w4_scales, gain, air, gT, offs, out
):
    nc = tc.nc
    with ExitStack() as ctx:
        keep = ctx.enter_context(tc.tile_pool(name="keep", bufs=1))
        ring = ctx.enter_context(tc.tile_pool(name="ring", bufs=2))
        shared = ctx.enter_context(tc.tile_pool(name="shared", bufs=1))
        psum = ctx.enter_context(tc.psum_pool(name="psum", bufs=1))

        def place(shape, dtype, name, tag=None):
            if name in PLACE:
                return shared.tile(shape, dtype, name=name, offset=PLACE[name], align_bytes=64)
            return keep.tile(shape, dtype, name=name, tag=tag or name, align_bytes=64)

        def bank(number):
            return psum.tile([P, HALF], F32, name="bank%d" % number)

        offsets = keep.tile([P, S // LIST_GROUP], U16, name="offsets")

        tab_plane = place([P, T], U8, "tab_plane")
        nc.gpsimd.memset(tab_plane[:].bitcast(I32), 0)
        gain_rows = keep.tile([P, PASS], F32, name="gain_rows")
        nc.gpsimd.memset(gain_rows[:], 0.0)
        air_rows = keep.tile([P, P], F32, name="air_rows", tag="air_rows", align_bytes=64)
        nc.gpsimd.memset(air_rows[:], 0.0)
        w4_plane = keep.tile([P, BLOCKS * N], U8, name="w4_plane", align_bytes=64)
        nc.gpsimd.memset(w4_plane[:].bitcast(I32), 0)

        w_raw, tab = {}, {}

        def load_w1(a):
            raw = place([P, 2, 2, H], F32, "w_raw%d0" % a)
            rows = w1[a * PASS : (a + 1) * PASS, :]
            nc.sync.dma_start(
                raw[:].rearrange("p u e c -> p (u e c)"), rows.rearrange("(p j) c -> p (j c)", j=PACK)
            )
            for b in range(BLOCKS):
                w_raw[a, b] = raw[:, :, :, b * PASS : (b + 1) * PASS]

        def load_last_w1(a):
            raw = place([P, 2, 2, H], F32, "w_raw%d0" % a)
            rows = w1[a * PASS : (a + 1) * PASS, :].rearrange("(p j) c -> p (j c)", j=PACK)
            for part in (slice(0, PACK * H - PASS), slice(PACK * H - PASS, PACK * H)):
                nc.sync.dma_start(raw[:].rearrange("p u e c -> p (u e c)")[:, part], rows[:, part])
            for b in range(BLOCKS):
                w_raw[a, b] = raw[:, :, :, b * PASS : (b + 1) * PASS]

        def load_tab(a):
            words = keep.tile([P, T], U32, name="tab%d" % a, tag="tab%d" % a, align_bytes=64)
            nc.sync.dma_start(
                words[:].bitcast(I32), tab_words[a].rearrange("p n i -> p (n i)").bitcast(I32)
            )
            tab[a] = words

        load_tab(0)
        nc.sync.dma_start(offsets[:], offs)
        load_tab(1)
        for q in reversed(range(QUADRANTS)):
            nc.sync.dma_start(
                tab_plane[QUADRANT * q : QUADRANT * q + PLANE_ROWS * PASSES, :].bitcast(I32),
                tab_scales[:, PLANE_ROWS * q : PLANE_ROWS * (q + 1), :].bitcast(I32),
            )
        load_w1(0)
        nc.sync.dma_start(gain_rows[0:BLOCKS, :], gain.rearrange("(b r) -> b r", b=BLOCKS))
        load_w1(1)
        load_tab(2)
        load_last_w1(2)

        readings = {}
        w4_codes = {}

        def load_w4(tiles):
            width = len(tiles) * FP4_BYTES * P
            codes = keep.tile([P, BLOCKS * width], U8, name="w4_codes%d" % tiles.start, align_bytes=64)
            start = tiles.start * FP4_BYTES * P
            nc.sync.dma_start(
                codes[:].bitcast(I32).rearrange("p (b w) -> p b w", b=BLOCKS),
                w4_words[:, :, start : start + width].bitcast(I32).rearrange("b p w -> p b w"),
            )
            for b in range(BLOCKS):
                for i, c in enumerate(tiles):
                    first = b * width + i * FP4_BYTES * P
                    w4_codes[b, c] = codes[:, first : first + FP4_BYTES * P]

        def load_w4_scales(quadrants):
            for q in quadrants:
                nc.sync.dma_start(
                    w4_plane[QUADRANT * q : QUADRANT * q + PLANE_ROWS, :]
                    .bitcast(I32)
                    .rearrange("r (b w) -> r b w", b=BLOCKS),
                    w4_scales[:, PLANE_ROWS * q : PLANE_ROWS * (q + 1), :].bitcast(I32).rearrange("b r w -> r b w"),
                )

        for i, c in enumerate(LOAD_ORDER):
            rows = keep.tile([P, T], F32, name="readings%d" % c)
            nc.sync.dma_start(rows[:], gT[c * P : (c + 1) * P, :])
            readings[c] = rows
            if i == W4_AFTER + 1:
                nc.sync.dma_start(air_rows[0:VIEW_TILES, :], air.rearrange("(c p) -> c p", p=P))
                load_w4_scales(range(0, QUADRANTS // 2))
        load_w4_scales(range(QUADRANTS // 2, QUADRANTS))
        load_w4(range(VIEW_TILES - 1, VIEW_TILES))
        load_w4(range(0, VIEW_TILES - 1))

        identity = keep.tile([P, P], F32, name="identity")
        make_identity(nc, identity[:])
        gain_bank = bank(BANKS - 1)
        for t in range(PACK):
            nc.tensor.transpose(gain_bank[:, t * P : (t + 1) * P], gain_rows[:, t:PASS:PACK], identity[:])
        gain_turned = gain_bank[:].rearrange("p (t b) -> p b t", t=PACK)[:, 0:BLOCKS, :]
        gain_work = keep.tile([P, 2, BLOCKS * PACK], F32, name="gain_work", tag="w_raw00", align_bytes=64)
        gain_rsqrt, gain_flat = gain_work[:, 0, :], gain_work[:, 1, :]
        nc.scalar.activation(gain_rsqrt.rearrange("p (b t) -> p b t", t=PACK), gain_turned, ACT.Abs_reciprocal_sqrt)
        nc.scalar.copy(gain_flat.rearrange("p (b t) -> p b t", t=PACK), gain_turned)
        gain_root = place([P, BLOCKS * PACK], F32, "gain_root")
        for col in range(BLOCKS * PACK):
            one = slice(col, col + 1)
            nc.scalar.activation(gain_root[:, one], gain_rsqrt[:, one], ACT.Copy, scale=gain_flat[:, one])


        w_codes, w_plane, v_words = {}, {}, {}

        def quantise_w1(a, blocks, shares):
            width = len(blocks) * PASS
            name = "%d%d" % (a, blocks[0])
            rounded = place([P, PACK * width], BF16, "rounded" + name, "rounded")
            for i, b in enumerate(blocks):
                part = rounded[:, i * PACK * PASS : (i + 1) * PACK * PASS]
                for copy, groups in shares[i]:
                    copy(
                        part.rearrange("p (t m u e) -> p m u e t", t=PACK, u=2, e=2)[:, groups],
                        w_raw[a, b].rearrange("p u e (m t) -> p m u e t", t=PACK)[:, groups],
                    )
            codes = place([P, width], U32, "w_codes" + name)
            plane = place([P, width], U8, "w_plane" + name)
            for i, b in enumerate(blocks):
                w_codes[a, b] = codes[:, i * PASS : (i + 1) * PASS]
                w_plane[a, b] = plane[:, i * PASS : (i + 1) * PASS]

            def quantise(first, last):
                nc.vector.quantize_mx(
                    out=codes[:, first * P : last * P].bitcast(FP8X4),
                    scales=plane[:, first * P : last * P],
                    in_=rounded[:, first * PASS : last * PASS],
                )

            return quantise

        def gather_words(passes):
            words = place([P, len(passes), S], U32, "v_words%d" % passes[0])
            for i, a in enumerate(passes):
                nc.vector.tensor_copy(words[:, i, :], tab[a][:].indirect(offsets[:]))
                for half in range(HALVES):
                    v_words[a, half] = words[:, i, half * HALF : (half + 1) * HALF]

        gather_words((0,))
        gather_words((1,))
        v_plane = keep.tile([P, S], U8, name="v_plane", align_bytes=64)
        nc.vector.tensor_copy(v_plane[:], tab_plane[:].indirect(offsets[:]))

        h_banks = {}

        def first_product(a, b, half, slots):
            cols = slice(half * HALF, (half + 1) * HALF)
            for t in slots:
                if a == 0:
                    h_banks[b, half, t] = bank(PACK * b + t)
                nc.tensor.matmul_mx(
                    out=h_banks[b, half, t][:],
                    lhsT=w_codes[a, b][:, t * P : (t + 1) * P].bitcast(FP8X4),
                    lhsT_scale=w_plane[a, b][:, t * P : (t + 1) * P],
                    rhs=v_words[a, half].bitcast(FP8X4),
                    rhs_scale=v_plane[PLANE_ROWS * a : P, cols],
                    start=(a == 0),
                    stop=(a == PASSES - 1),
                )

        z_rows, z_woven, z_codes, z_plane = {}, {}, {}, {}

        def energies(b, half, slots):
            name = "z_rows%d%d" % (b, half)
            if (b, half) in z_rows:
                rows = z_rows[b, half]
            else:
                rows = place([P, PACK, HALF], BF16, name, "w_raw10")
            for t in slots:
                col = PACK * b + t
                nc.scalar.activation(
                    rows[:, t, :], h_banks[b, half, t][:], ACT.Square, scale=gain_root[:, col : col + 1]
                )
            z_rows[b, half] = rows

        def weave_z(b, half):
            if b == 0:
                z_woven[half] = keep.tile(
                    [P, BLOCKS * PACK * HALF], BF16, name="z_woven%d" % half, tag=("w_raw00", "tab0")[half], align_bytes=64
                )
            nc.scalar.copy(
                z_woven[half][:, b * PACK * HALF : (b + 1) * PACK * HALF].rearrange(
                    "p (c i t) -> p c t i", i=RUN, t=PACK
                ),
                z_rows[b, half][:].rearrange("p t (c i) -> p c t i", i=RUN),
            )

        def quantise_z(half, calls):
            codes = keep.tile([P, BLOCKS * HALF], U32, name="z_codes%d" % half, align_bytes=64)
            tag = "air_rows" if half == 0 else "first_inverse"
            plane = keep.tile([P, BLOCKS * HALF], U8, name="z_plane%d" % half, tag=tag, align_bytes=64)
            width = BLOCKS * HALF // calls
            for first in range(0, BLOCKS * HALF, width):
                nc.vector.quantize_mx(
                    out=codes[:, first : first + width].bitcast(FP8X4),
                    scales=plane[:, first : first + width],
                    in_=z_woven[half][:, PACK * first : PACK * (first + width)],
                )
            z_codes[half], z_plane[half] = codes, plane

        picked = {}

        def gather_readings():
            early = place([P, EARLY_TILES, S], F32, "picked")
            late = place([P, VIEW_TILES - EARLY_TILES, S], F32, "picked_late")
            for i, c in enumerate(LOAD_ORDER):
                picked[c] = early[:, i, :] if i < EARLY_TILES else late[:, i - EARLY_TILES, :]
                nc.vector.tensor_copy(picked[c], readings[c][:].indirect(offsets[:]))

        inverse = {}

        def second_product(c, half, numbers):
            width = HALF // len(numbers)
            if half == 0 and c in SPLIT_TILES[:AHEAD]:
                root = keep.tile([P, HALF], F32, name="first_root", tag="tab0", align_bytes=64)
            else:
                name = "root%d%d" % (c, half)
                root = shared.tile([P, HALF], F32, name=name, offset=PLACE["z_rows01"], align_bytes=64)
            if (c, half) == (SPLIT_TILES[0], 0):
                whole = keep.tile([P, HALF], F32, name="first_inverse", tag="first_inverse", align_bytes=64)
                inverse[c, half] = whole[:]
            elif c in SPLIT_TILES:
                whole = ring.tile([P, HALF], F32, name="inverse_half", bufs=INVERSE_TILES)
                inverse[c, half] = whole[:]
            elif half == 0:
                whole = ring.tile([P, S], F32, name="inverse")
                inverse[c] = whole[:]
                inverse[c, 0], inverse[c, 1] = whole[:, 0:HALF], whole[:, HALF:S]
            for i, number in enumerate(numbers):
                y_bank = bank(number)
                for b in range(BLOCKS):
                    first = b * N + c * P
                    entries = slice(b * HALF + i * width, b * HALF + (i + 1) * width)
                    nc.tensor.matmul_mx(
                        out=y_bank[:, 0:width],
                        lhsT=w4_codes[b, c].bitcast(FP4X4),
                        lhsT_scale=w4_plane[:, first : first + P],
                        rhs=z_codes[half][:, entries].bitcast(FP8X4),
                        rhs_scale=z_plane[half][:, entries],
                        start=(b == 0),
                        stop=(b == BLOCKS - 1),
                    )
                nc.scalar.activation(
                    root[:, i * width : (i + 1) * width],
                    y_bank[:, 0:width],
                    ACT.Abs_reciprocal_sqrt,
                    bias=air_cols[:, c : c + 1],
                )
            for i in range(len(numbers)):
                part = slice(i * width, (i + 1) * width)
                nc.scalar.activation(inverse[c, half][:, part], root[:, part], ACT.Square)

        def scatter(c, halves):
            start, stop = halves.start * HALF, halves.stop * HALF
            nc.vector.tensor_tensor(
                readings[c][:].indirect(offsets[:, start // LIST_GROUP : stop // LIST_GROUP]),
                picked[c][:, start:stop],
                inverse[c, halves.start] if len(halves) == 1 else inverse[c],
                MULT,
            )

        def store(c):
            nc.sync.dma_start(out[c * P : (c + 1) * P, :], readings[c][:])

        on_scalar = [(nc.scalar.copy, slice(0, P))]
        on_vector = [(nc.vector.tensor_copy, slice(0, P))]

        def on_both(groups):
            return [(nc.vector.tensor_copy, slice(0, groups)), (nc.scalar.copy, slice(groups, P))]

        quantise_w1(0, (0, 1), (on_scalar, on_vector))(0, 2 * PACK)
        quantise = quantise_w1(1, (0, 1), (on_scalar, on_vector))
        quantise(PACK, 2 * PACK)
        gather_words((2,))
        quantise(0, PACK)
        for a in range(PASSES):
            for b in range(BLOCKS):
                if a == PASSES - 1:
                    quantise = quantise_w1(a, (b,), (on_both(VECTOR_GROUPS[b]),))
                    step = PACK // 2 if b == 0 else PACK
                    for first in range(0, PACK, step):
                        quantise(first, first + step)
                first_product(a, b, 0, range(PACK))
        energies(0, 0, range(PACK))
        energies(1, 0, range(PACK))
        weave_z(0, 0)
        weave_z(1, 0)

        air_cols = keep.tile([P, VIEW_TILES], F32, name="air_cols")
        air_bank = bank(BANKS - 1)
        nc.tensor.transpose(air_bank[:, 0:P], air_rows[:], identity[:])
        nc.scalar.copy(air_cols[:], air_bank[:, 0:VIEW_TILES])
        quantise_z(0, BLOCKS)

        for b in range(BLOCKS):
            for t in range(PACK):
                for a in range(PASSES):
                    first_product(a, b, 1, (t,))
        gather_readings()
        energies(0, 1, range(PACK))
        energies(1, 1, range(PACK))

        second_product(SPLIT_TILES[0], 0, (0, 1))
        scatter(SPLIT_TILES[0], range(0, 1))
        second_product(SPLIT_TILES[1], 0, (2,))
        scatter(SPLIT_TILES[1], range(0, 1))
        weave_z(0, 1)
        weave_z(1, 1)
        quantise_z(1, 1)
        second_product(SPLIT_TILES[2], 0, (3,))
        scatter(SPLIT_TILES[2], range(0, 1))

        next_bank = PACK
        for i, c in enumerate(SPLIT_TILES):
            count = 2 if i == 0 else 1
            second_product(c, 1, range(next_bank, next_bank + count))
            next_bank = next_bank + count
            scatter(c, range(1, HALVES))
            store(c)
        for c in range(VIEW_TILES - len(SPLIT_TILES)):
            for half in range(HALVES):
                second_product(c, half, (next_bank % BANKS,))
                next_bank = next_bank + 1
            scatter(c, range(0, HALVES))
            store(c)
